import numpy as np, ml_dtypes
CORES = [66,74,82,90,194,202,210,218]
N = 8
import mx_ref
BF = ml_dtypes.bfloat16
def gentries(a):
    return np.ascontiguousarray(a.reshape(8, 16, -1).transpose(0, 2, 1)).reshape(8, -1)
def gtable(e):
    e = np.asarray(e); return np.ascontiguousarray(e.reshape(8, -1, 16).transpose(0, 2, 1)).reshape(128, -1).astype(np.int32)
def gcols(t, e):
    v = np.concatenate([t.reshape(8, 16, -1, 4), np.zeros((8, 16, 1, 4), BF)], axis=2)
    return np.ascontiguousarray(np.stack([v[g][:, e[g]] for g in range(8)])).reshape(128, -1)
def tile(rs):
    return np.stack(rs, axis=2).reshape(128, -1).astype(BF)
def cut(t, i, w=512):
    return t[:, w * i:w * i + w]
def pick(q, e):
    c = np.concatenate([q[0].reshape(128, -1, 4), np.zeros((128, 1, 4), np.uint8)], axis=1); s = np.concatenate([q[1], np.ones((16, 1), np.uint8)], axis=1)
    return (np.ascontiguousarray(c[:, e].reshape(128, -1)), np.ascontiguousarray(s[:, e]))
def join(*qs):
    return (np.concatenate([q[0] for q in qs], axis=1), np.concatenate([q[1] for q in qs], axis=1))
def put(q, e, v):
    c, s = q[0].reshape(128, -1, 4).copy(), q[1].copy(); c[:, e] = v[0].reshape(128, -1, 4); s[:, e] = v[1]
    return (c.reshape(128, -1), s)
def pk(c, s):
    return (np.ascontiguousarray(c), mx_ref.live(s))
def emit(q):
    return q[0], q[1]
def packed(v, rng):
    q = [mx_ref.quantize(np.ascontiguousarray(v[r])) for r in range(N)]
    return np.stack([a for a, b in q]), np.stack([mx_ref.plane(b, rng) for a, b in q])
def values_of_codes():
    e, c = np.zeros((128, 128, 4), np.float32), np.zeros((128, 2, 4), np.uint8)
    e[np.arange(128), np.arange(128), 0] = 1
    c[:127, :, 0] = np.arange(256).reshape(2, 128).T[:127]
    return mx_ref.matmul(mx_ref.quantize(e.reshape(128, 512).astype(BF)), (c.reshape(128, 8), np.full((16, 2), 127, np.uint8))).T.reshape(-1).astype(np.float64)
CODE_VALUE, SCALE_VALUE = values_of_codes(), 2.0 ** (np.arange(256) - 127.0)
def decode(q):
    return (CODE_VALUE[q[0]].reshape(16, 8, -1, 4) * SCALE_VALUE[q[1]][:, None, :, None] + 0.0).reshape(128, -1).astype(np.float32)
def f(rng, *shape):
    return mx_ref.flush((rng.standard_normal(shape, dtype=np.float32) * np.exp2(rng.integers(-2, 3, shape[:-1] + (1,)))).astype(BF))
def wide(rng, *shape, cols=0):
    v = rng.standard_normal(shape, dtype=np.float32) * np.exp2(rng.integers(-12, 13, shape)).astype(np.float32)
    if cols: v *= np.repeat(np.exp2(rng.integers(-cols, cols + 1, shape[:-2] + (1, shape[-1] // 4))) * (rng.random(shape[:-2] + (1, shape[-1] // 4)) > 0.0625), 4, axis=-1).astype(np.float32)
    return mx_ref.flush(v.astype(BF))
C, A, R = 352, 160, 3
STEP = [4, 2, 1]
def layout(bad, sz, pr):
    g, n = np.arange(8)[:, None], np.arange(C)
    p = np.bitwise_xor.accumulate(np.concatenate([np.zeros((8, 1), np.int64), bad], axis=1), axis=1)
    odd = np.concatenate([p[g, n + sz] != p[g, n], np.zeros((8, 1), bool)], axis=1)
    up = np.where(pr < 0, C, pr)
    end = np.where(pr < 0, 0, pr + sz[g, pr])
    sib = np.where(n > pr + 1, pr + 1, np.where(n + sz < end, n + sz, C))
    pair = odd[:, :C] & odd[g, sib]
    top = np.where(odd[:, :C] & odd[g, up] & ~pair, up, n)
    for i in range(9): top = top[g, top]
    other = np.where(pair, sib, n)[g, top]
    name, rise = np.minimum(top, other), top < other
    begin = np.zeros((8, C), np.int64)
    np.maximum.at(begin, (g, name), np.where(rise, n, name))
    key = np.where(odd[:, :C], begin[g, name] * 2 * C + np.where(rise, C - 1 - n, C + n), 2 * C * C + n)
    o = np.argsort(key, axis=1, kind="stable")
    same = name[g, o[:, :-1]] == name[g, o[:, 1:]]
    return o, np.concatenate([np.where(same, o[:, 1:], -1), np.full((8, 1), -1)], axis=1)
def differences(t, o, follow):
    return (gcols(t, o).astype(np.float32) - gcols(t, follow).astype(np.float32)).astype(BF)
def big(v):
    v = v.astype(np.float32)
    v[np.abs(v) < np.float32(2.0 ** -16)] = 0
    return v.astype(BF)
def numbers_of(rng):
    return {"x": big(f(rng, N, 128, 4 * C)), "u": np.array(f(rng, N, 128, 512)), "v": np.array(f(rng, N, 128, 512))}
def weights(rng, still=[]):
    w = big(f(rng, N, 128, 2048)).reshape(N, 8, 16, 4, 8, 16, 4)
    for i in still:
        w[:, :, i] = 0
        w[:, :, :, :, :, i] = 0
    c, p = packed(np.ascontiguousarray(w).reshape(N, 128, 2048), rng)
    return {"wc": c, "ws": p}
def grown(rng):
    a, kids, way = [-1] * C, [0] * C, [0]
    back = (rng.geometric(rng.choice([0.4, 0.6, 0.8, 0.95]), C) - 1).tolist()
    for n in range(1, C):
        del way[max(1, len(way) - back[n]):]
        p = way[-1]
        a[n] = p
        kids[p] += 1
        if kids[p] == 2: way.pop()
        way.append(n)
    return np.array(a)
def chain():
    return np.arange(C) - 1
def fork(h):
    a = np.arange(C) - 1
    a[h] = 0
    return a
def comb():
    a = (np.arange(C) - 1) // 2 * 2
    a[0] = -1
    return a
def rake():
    n, h = np.arange(C), C // 2 + 1
    return np.where(n < h, n - 1, 2 * h - 2 - n)
def halves():
    a, todo = np.zeros(C, np.int64), [(0, C, -1)]
    while todo:
        lo, hi, p = todo.pop()
        a[lo] = p
        m = lo + 1 + (hi - lo) // 2
        if m > lo + 1: todo.append((lo + 1, m, lo))
        if hi > m: todo.append((m, hi, lo))
    return a
def trees(rng):
    return np.stack([np.stack([grown(rng) for g in range(8)]) for r in range(N)])
def stored(a):
    k, i = a.reshape(8 * N, C), np.arange(8 * N)
    s = np.ones((8 * N, C), np.int64)
    for n in range(C - 1, 0, -1): s[i, k[:, n]] += s[:, n]
    return {"sz": np.stack([gtable(e) for e in s.reshape(N, 8, C)]), "pr": np.stack([gtable(e) for e in a])}
def planted(rng, a, bad, still=[0]):
    d = numbers_of(rng)
    x = d["x"].reshape(N, 8, 16, C, 4)
    x[:, :, 0] = 0
    x[:, :, 0, :, 0] = np.where(bad, 1.0, -1.0).astype(np.float32).astype(BF)
    u = d["u"].reshape(N, 128, 128, 4)
    u[:, :, ::16] = 0
    for h in range(0, 128, 16): u[:, h, h, 0] = 1
    return {"x": x.reshape(N, 128, 4 * C), "u": u.reshape(N, 128, 512), "v": d["v"], **weights(rng, still), **stored(a)}
def setup_inputs(rng):
    return {**numbers_of(rng), **weights(rng), **stored(trees(rng))}
def setup_inputs_zeros(rng):
    d = numbers_of(rng)
    x = d["x"].reshape(N, 8, 16, C, 4)
    u = d["u"].reshape(N, 128, 128, 4)
    u[:, :, ::16] = 0
    e = rng.permutation(N)
    for i in range(N):
        r, body, by = e[i], np.zeros((8, 4)), np.zeros((8, 4))
        if i % 2:
            body[:] = 2.0 ** 26
            by[:] = 2.0 ** 30
        else:
            body[:2, 0] = [9 * 2.0 ** -33, 10 * 2.0 ** -33]
            by[:2, 0] = [9 * 2.0 ** -33, -8 * 2.0 ** -33]
        m = np.stack([rng.permutation(C) % 3 - 1.0 for g in range(8)])
        if i == 0: m[:] = 1
        z = m[:, None, :, None] * body[None, :, None, :]
        x[r][:, :8] = z.astype(np.float32).astype(BF)
        k = by.astype(np.float32).astype(BF)
        for h in range(0, 128, 16): u[r, h:h + 8, h] = k
    x[e[1]] = 0
    return {"x": x.reshape(N, 128, 4 * C), "u": u.reshape(N, 128, 512), "v": d["v"], **weights(rng, range(8)), **stored(trees(rng))}
def setup_inputs_chains(rng):
    a = np.broadcast_to(chain(), (N, 8, C)).copy()
    bad = np.zeros((N, 8, C), bool)
    h, e = int(rng.integers(8)), int(rng.integers(N))
    for r in range(N):
        k = np.insert(rng.permutation(np.delete(np.arange(8), h)), 5, h)
        for i, n in enumerate([1, A - 1, A, A + 1, C - 1, C]): bad[r, k[i], n - 1] = True
        bad[r, k[6]] = True
    d = planted(rng, a, bad, [0, 8])
    d["x"].reshape(N, 8, 16, C, 4)[e, h, 8, :, 0] = np.where(np.arange(C) % 2 == 1, -2.0 ** 28, 2.0 ** 28).astype(np.float32).astype(BF)
    d["v"][:, 16 * h + 8] = 0
    return d
def setup_inputs_forks(rng):
    a, bad = np.zeros((N, 8, C), np.int64), np.zeros((N, 8, C), bool)
    for r in range(N):
        k = rng.permutation(8)
        for i, h in enumerate([2, A, A + 1, C - 1]):
            a[r, k[i]] = fork(h)
            bad[r, k[i], [h - 1, C - 1]] = True
        bad[r, k[1], 0] = True
        for i, b in enumerate([comb(), rake(), halves()]):
            a[r, k[4 + i]] = b
            bad[r, k[4 + i]] = ~np.isin(np.arange(C), b)
        a[r, k[7]] = grown(rng)
        bad[r, k[7]] = True
    return planted(rng, a, bad)
def setup_inputs_spread(rng):
    d = setup_inputs(rng)
    d["x"] = big(wide(rng, N, 128, 4 * C, cols=6))
    return d
def check_inputs(d):
    b = []
    for k in ("x", "u", "v"):
        a = np.abs(d[k].astype(np.float32))
        if not (np.isfinite(a).all() and ((a == 0) | (a >= 2.0 ** -30) & (a <= 2.0 ** 30)).all()): b.append("a value of " + k)
    none, least, most = [emit(mx_ref.quantize(np.full((128, 16), k, np.float32).astype(BF)))[1][0, 0] for k in (0.0, 2.0 ** -30, 2.0 ** 30)]
    g, n = np.arange(8)[:, None], np.arange(C)
    for r in range(N):
        if ((d["wc"][r] == 0x7F) | (d["wc"][r] == 0xFF)).any(): b.append("wc: a code that is no number")
        s = mx_ref.live(d["ws"][r])
        if ((s != none) & ((s < least) | (s > most))).any(): b.append("ws: a scale out of range")
        s, p = gentries(d["sz"][r]).astype(np.int64), gentries(d["pr"][r]).astype(np.int64)
        e = n + s
        if (s < 1).any() or (e > C).any() or (s[:, 0] != C).any(): b.append("sz: a size out of range")
        above = np.max(np.where((n[:, None] < n) & (e[:, :, None] > n), n[:, None], -1), axis=1)
        if (above != p).any(): b.append("pr: not the parent")
        elif (e > e[g, np.maximum(p, 0)]).any(): b.append("sz: a subtree that goes beyond the parent's")
        elif np.max(np.sum(p[:, :, None] == n, axis=1)) > 2: b.append("pr: more than two children")
    return b
def reference(x, u, v, wc, ws, sz, pr):
    qu = [mx_ref.quantize(u[r]) for r in range(N)]
    lay = [pk(wc[r], ws[r]) for r in range(N)]
    now = [x[r] for r in range(N)]
    for t in range(R):
        sent, paths = [], []
        for r in range(N):
            q = mx_ref.quantize(now[r])
            p = mx_ref.matmul(qu[r], q)
            sent.append(q)
            paths.append(layout(p[::16] > 0, gentries(sz[r]), gentries(pr[r])))
        came = decode(join(*sent)).astype(BF)
        made = []
        for r in range(N):
            e = (r - STEP[t]) % N
            z = np.concatenate([differences(cut(came, e, 4 * C), *paths[e])[:, :4 * A], differences(now[r], *paths[r])[:, 4 * A:]], axis=1)
            q = mx_ref.quantize(np.ascontiguousarray(z))
            made.append(tile([mx_ref.matmul(pick(lay[r], np.arange(128 * b, 128 * b + 128)), q) * np.float32(0.0078125) + z[:, b::4].astype(np.float32) for b in range(4)]))
        now = made
    y, ot = np.zeros((N, 128, C), np.float32), np.zeros((N, 8, C), np.float32)
    oc, osc = np.zeros((N, 128, 4 * C), np.uint8), np.zeros((N, 16, C), np.uint8)
    for r in range(N):
        q = mx_ref.quantize(now[r])
        y[r] = mx_ref.matmul(mx_ref.quantize(v[r]), q)
        ot[r] = paths[r][0]
        oc[r], osc[r] = emit(q)
    return {"y": y, "ot": ot, "oc": oc, "osc": osc}

@@ -1,0 +1,474 @@
+import numpy as np
+from concourse.mybir import dt, AluOpType as Op, AxisListType, ActivationFunctionType as Fn
+
+C, A, R = 352, 160, 3
+STEP = [4, 2, 1]
+K = C // 16
+PL = 368
+OFF = 12582912.0
+SL = 4 * C + 8
+BIG = 2048.0
+F, B16, H16, I, U16, Q, S8 = "float32", "bfloat16", "float16", "int32", "uint16", "float8_e4m3fn_x4", "uint8"
+
+_S = {
+    "szi": (K, I), "pri": (K, I), "xt": (4 * C, B16), "ut": (512, B16), "vt": (512, B16),
+    "qw": (512, Q), "sw": (512, S8), "qu": (128, Q), "su": (128, S8), "qr": (128, Q), "sr": (128, S8),
+    "qv": (128, Q), "sv": (128, S8), "ew": (520, B16), "ones": (520, B16), "qe": (512, Q), "se": (512, S8),
+    "qz": (C, Q), "zs": (C, S8), "zt": (4 * C, B16), "z128": (4 * C, B16), "tf": (4 * C, F),
+    "xp": (4 * PL, B16), "yp": (4 * PL, B16), "fl": (4 * 176, B16), "fo": (4 * 208, B16),
+    "iot": (360, F), "iw2": (708, F), "m16": (16, F), "dm": (C, F), "dmb": (C, B16), "dmh": (C, B16),
+    "m8": (736, B16), "twos": (C, B16), "nn": (64, F),
+    "col": (32, F), "coli": (16, I), "cst": (16 * K, F), "csti": (K, I), "su16": (8 * K, U16),
+    "r1": (C, F), "r2": (C, F), "r3": (C, F), "r4": (C, F), "r5": (C, F), "n2": (C, F), "nf": (C, F),
+    "mm": (C, H16), "d0": (C, H16), "hold": (C, B16), "ops": (C, B16), "junk": (4048, B16),
+    "pay": (C, F), "bt": (SL + C, F), "td": (SL, F), "c2t": (4 * C, F), "vtb": (4 * C, F),
+    "bb": (C, B16), "hh": (C, B16), "pp": (PL, B16), "pq": (PL, B16), "oo": (C, B16), "d1": (C, B16), "vv": (C, F),
+    "gg": (C, H16), "uu": (384, H16), "tt": (736, H16), "rr": (736, H16), "r8": (96, F), "zi": (64, I),
+    "wd": (C, B16), "sl": (24 * K, F), "sli": (4 * K, I), "lb": (5 * K, F), "lu": (8 * K, U16),
+    "c1": (C, F), "c3": (C, F), "gb": (C, F), "vr": (C, F), "ga": (2 * C, F), "c2": (2 * C, F), "jj": (712, F),
+    "gf": (C, H16), "wh": (C, H16), "w": (C, F), "vo": (C, F), "otr": (C, F), "yo": (C, F),
+}
+for _t in range(R + 1):
+    _S["qx%d" % _t] = (C, Q)
+    _S["sx%d" % _t] = (C, S8)
+for _t in range(R):
+    _S["lq%d" % _t] = (C, Q)
+    _S["ls%d" % _t] = (C, S8)
+    _S["ll%d" % _t] = (32, U16)
+    _S["lo%d" % _t] = (2 * K, U16)
+SCRATCH = {k: ("sbuf", [128, n], d) for k, (n, d) in _S.items()}
+SCRATCH["ps"] = ("psum", [128, 4096], "float32")
+NDMA = 20
+SEMAPHORES = (["cv", "ca", "ct", "cg", "sent"] + ["dma%d" % i for i in range(NDMA)]
+              + ["big%d" % t for t in range(R)] + ["lst%d" % t for t in range(R)])
+
+
+def rank_program(g, core, T, topo):
+    rank = T.rank_of(core)
+    if rank is None:
+        return
+    N = len(T.cores)
+    eng = {"v": g.vector, "a": g.scalar, "t": g.tensor, "g": g, "s": g.sync}
+    own = {"v": "cv", "a": "ca", "t": "ct", "g": "cg"}
+    count = {}
+    clock = {q: {} for q in eng}
+    events = [None]
+    width = {k: v[1][1] for k, v in SCRATCH.items()}
+    width["ps"] = 8
+    wr = {k: np.zeros(n, np.int64) for k, n in width.items()}
+    rd = {k: {} for k in width}
+    ndma = [0]
+
+    def V(name, a=0, b=None, s=1):
+        b = SCRATCH[name][1][1] if b is None else b
+        ap = T[name][:, a:b] if s == 1 else T[name][:, a:b:s]
+        if name == "ps":
+            return (ap, name, np.arange(a // 512, (b - 1) // 512 + 1))
+        return (ap, name, np.arange(a, b, s))
+
+    def X(win, off):
+        return (win[0].indirect(off[0]), win[1], win[2], off)
+
+    def wait(q, e):
+        sem, val, seen = events[e]
+        if clock[q].get(sem, 0) < val:
+            eng[q].wait_ge(T.sem[sem], val)
+            clock[q][sem] = val
+        for k, x in seen.items():
+            if clock[q].get(k, 0) < x:
+                clock[q][k] = x
+
+    def issue(q, call, outs, ins, sem=None, inc=1, direct=False):
+        reads, writes = [], []
+        for v in ins:
+            if isinstance(v, tuple):
+                (writes if v[1] == "ps" else reads).append(v)
+                if len(v) == 4:
+                    reads.append(v[3])
+        for v in outs:
+            writes.append(v)
+            if len(v) == 4:
+                reads.append(v[3])
+        need = set()
+        for v in reads + writes:
+            need.update(np.unique(wr[v[1]][v[2]]).tolist())
+        for v in writes:
+            for arr in rd[v[1]].values():
+                need.update(np.unique(arr[v[2]]).tolist())
+        need.discard(0)
+        for e in sorted(need, reverse=True):
+            wait(q, e)
+        sem = own[q] if sem is None else sem
+        made = call()
+        if not direct:
+            made.then_inc(T.sem[sem], inc)
+        count[sem] = count.get(sem, 0) + inc
+        events.append((sem, count[sem], dict(clock[q])))
+        e = len(events) - 1
+        for v in reads:
+            if sem not in rd[v[1]]:
+                rd[v[1]][sem] = np.zeros(width[v[1]], np.int64)
+            rd[v[1]][sem][v[2]] = e
+        for v in writes:
+            wr[v[1]][v[2]] = e
+
+    def ap(x):
+        return x[0] if isinstance(x, tuple) else x
+
+    def cp(o, i):
+        issue("v", lambda: g.vector.tensor_copy(o[0], i[0]), [o], [i])
+
+    def tt(o, a, b, op):
+        issue("v", lambda: g.vector.tensor_tensor(o[0], a[0], b[0], op), [o], [a, b])
+
+    def ts(o, a, s1, op0, s2=None, op1=None):
+        if op1 is None:
+            issue("v", lambda: g.vector.tensor_scalar(o[0], a[0], ap(s1), None, op0), [o], [a, s1])
+        else:
+            issue("v", lambda: g.vector.tensor_scalar(o[0], a[0], ap(s1), ap(s2), op0, op1), [o], [a, s1, s2])
+
+    def scan(o, a, b, init, op0, op1):
+        issue("v", lambda: g.vector.tensor_tensor_scan(o[0], a[0], b[0], ap(init), op0, op1), [o], [a, b, init])
+
+    def fill(o, x):
+        issue("v", lambda: g.vector.memset(o[0], x), [o], [])
+
+    def act(o, i, fn=Fn.Identity, bias=0.0, scale=1.0, acc=None):
+        if acc is None:
+            issue("a", lambda: g.scalar.activation(o[0], i[0], fn, bias=ap(bias), scale=ap(scale)), [o], [i, bias, scale])
+        else:
+            issue("a", lambda: g.scalar.activation(o[0], i[0], fn, bias=ap(bias), scale=ap(scale), accum_out=acc[0]),
+                  [o, acc], [i, bias, scale])
+
+    def quant(q, s, a, b, tile, at=None):
+        at = 4 * a if at is None else at
+        o, p, i = V(q, a, b), V(s, a, b), V(tile, at, at + 4 * (b - a))
+        issue("v", lambda: g.vector.quantize_mx(o[0], p[0], i[0]), [o, p], [i])
+
+    def mm(bank, lq, ls, at, rq, rs, a, b):
+        o = V("ps", 512 * bank, 512 * bank + b - a)
+        w, ws, x, xs = V(lq, at, at + 128), V(ls, at, at + 128), V(rq, a, b), V(rs, a, b)
+        issue("t", lambda: g.tensor.matmul_mx(o[0], w[0], ws[0], x[0], xs[0], True, True), [o], [w, ws, x, xs])
+
+    def iota(o, pattern, base, cm):
+        if SCRATCH[o[1]][2] == I:
+            issue("g", lambda: g.iota(o[0], pattern, base, cm), [o], [])
+        else:
+            issue("g", lambda: g.iota(o[0], pattern, base, cm, allow_small_or_imprecise_dtypes=True), [o], [])
+
+    def dma(q, out, in_, outs, ins):
+        ndma[0] += 1
+        issue(q, lambda: eng[q].dma_start(out, in_), outs, ins, sem="dma%d" % (ndma[0] - 1), inc=16)
+
+    def send(dst, to, src, sem, codes=False):
+        rid, pid = topo.addr(dst, core)
+        mask, n = topo.mask(core, dst), len(topo.engines(core, dst))
+        o, i = (to[0].bitcast(dt.uint8), src[0].bitcast(dt.uint8)) if codes else (to[0], src[0])
+        issue("g", lambda: g.remote_dma(o, i, T.sem[sem], T.sem.sent, pid, rid, mask), [], [src], sem="sent", inc=n, direct=True)
+
+    def arrives(sem, total, views):
+        count[sem] = total
+        events.append((sem, total, {}))
+        for v in views:
+            wr[v[1]][v[2]] = len(events) - 1
+
+    def col(i):
+        return V("col", i, i + 1)
+
+    def coli(i):
+        return V("coli", i, i + 1)
+
+    def L(name, i, n=1):
+        return V(name, K * i, K * (i + n))
+
+    def diag(name):
+        return V(name, 15, C, 16)
+
+    dma("s", T.szi[:], T.sz[:], [V("szi")], [])
+    dma("a", T.xt[:], T.x[:], [V("xt")], [])
+    dma("s", T.pri[:], T.pr[:], [V("pri")], [])
+    dma("s", T.ut[:], T.u[:], [V("ut")], [])
+    dma("s", T.qw[:].bitcast(dt.uint8), T.wc[:], [V("qw")], [])
+    dma("s", T.sw[:], T.ws[:], [V("sw")], [])
+    dma("s", T.vt[:], T.v[:], [V("vt")], [])
+
+    iw = V("iot")
+    iota(coli(0), [[0, 1]], 0, 1)
+    iota(L("cst", 0), [[16, K]], 0, 0)
+    iota(V("m16"), [[1, 16]], 0, 0)
+    iota(iw, [[1, 360]], 0, 0)
+    iota(V("iw2"), [[4, 354], [1, 2]], 0, 0)
+    iota(V("col", 24, 28), [[1, 2], [32, 2]], 0, 0)
+    iota(V("m8"), [[0, 92], [1, 8]], 0, 0)
+    iota(V("td"), [[0, SL]], 0, 0)
+    iota(V("c2", C, 2 * C), [[0, C]], 0, 0)
+    fill(V("ones"), 1.0)
+    fill(V("twos"), -2.0)
+    act(V("bt", 0, SL, 4), V("ones", 0, 354), scale=0.0)
+    act(V("bt", 1, SL, 4), V("ones", 0, 354), scale=0.0)
+    fill(V("r8", 8, 16), 2.0)
+    ts(coli(1), coli(0), 15, Op.bitwise_and)
+    ts(coli(2), coli(0), 7, Op.bitwise_and)
+    ts(coli(3), coli(0), 3, Op.arith_shift_right, 1, Op.bitwise_and)
+    ts(coli(4), coli(0), 4, Op.arith_shift_right)
+    scan(V("r8", 0, 8), V("r8", 8, 16), V("ones", 0, 8), 0.5, Op.mult, Op.add)
+    cp(V("col", 0, 3), V("coli", 1, 4))
+    tt(coli(5), coli(4), coli(0), Op.add)
+    nL = L("cst", 1)
+    nbias, dum, n4, evn, koff, kthr, nk, dep = (L("cst", i) for i in (2, 3, 4, 5, 6, 7, 8, 9))
+    szu, paru, endu, e1u, depu, pmu = (L("su16", i) for i in range(6))
+    pick, rep = V("su16", 6 * K, 6 * K + 4), V("su16", 7 * K, 7 * K + 8)
+    ts(nL, L("cst", 0), col(0), Op.add)
+    ts(col(9), col(2), -2.0, Op.mult, 5.0, Op.add)
+    ts(col(10), col(2), 4.0, Op.mult)
+    ts(col(11), col(2), 6.0, Op.mult)
+    ts(col(12), col(0), 15.0, Op.is_lt, BIG, Op.mult)
+    ts(coli(6), coli(5), 1, Op.bitwise_and)
+    ts(pmu, L("cst", 0), 0.0, Op.mult, col(0), Op.add)
+    cp(rep, V("cst", 0, 8))
+    ts(V("r8", 16, 24), V("m16", 0, 8), col(1), Op.is_equal)
+    ts(V("r8", 32, 48), V("m16"), col(0), Op.subtract)
+    act(V("n2"), V("iot", 0, C), scale=col(10), bias=col(11))
+    act(nbias, nL, scale=-1.0, bias=-0.5)
+    ts(col(15), col(0), 0.5, Op.mult, -8.0, Op.add)
+    tt(V("r8", 24, 32), V("r8", 0, 8), V("r8", 16, 24), Op.mult)
+    ts(V("r8", 48, 64), V("r8", 32, 48), 0.0, Op.is_equal, 4 * BIG, Op.mult)
+    ts(V("r8", 64, 80), V("r8", 32, 48), 1.0, Op.is_equal, -BIG, Op.mult)
+    ts(col(8), col(9), 4096.0, Op.mult)
+    issue("v", lambda: g.vector.tensor_reduce(col(5)[0], V("r8", 24, 32)[0], AxisListType.X, Op.add), [col(5)], [V("r8", 24, 32)])
+    tt(V("m16"), V("r8", 48, 64), V("r8", 64, 80), Op.add)
+    ts(col(13), col(12), -1.0 / 64, Op.mult, -4.0, Op.add)
+    ts(col(6), col(5), -1.5, Op.mult)
+    ts(col(7), col(5), 0.5, Op.mult)
+    ts(col(16), col(5), -0.5, Op.add)
+    act(koff, nL, scale=0.5, bias=col(15))
+    act(V("nf"), V("iot", 0, C), scale=1.0 / 1024)
+    act(V("dmb"), X(V("m16"), pmu), scale=1.0 / 64)
+
+    cp(szu, V("szi"))
+    tt(V("csti"), V("szi"), nL, Op.add)
+    cp(paru, V("pri"))
+    ts(L("cst", 10), V("pri"), 1.0, Op.add)
+    ts(L("cst", 11), V("pri"), 2.0, Op.mult, 4.0, Op.add)
+    cp(endu, V("csti"))
+    act(V("r2"), X(iw, szu), Fn.Abs, bias=col(6))
+    act(V("r3"), X(iw, szu))
+    act(V("r5"), X(iw, endu))
+    tt(L("cst", 10), L("cst", 10), nL, Op.not_equal)
+    ts(L("cst", 12), V("szi"), col(5), Op.is_ge, col(9), Op.mult)
+    ts(L("cst", 13), V("szi"), 0.5, Op.mult, col(5), Op.is_le)
+    tt(L("cst", 11), L("cst", 11), L("cst", 10), Op.add)
+    tt(L("cst", 12), L("cst", 12), L("cst", 13), Op.mult)
+    cp(e1u, L("cst", 11))
+    ts(kthr, L("cst", 12), col(13), Op.add)
+    fill(V("pp", 0, 1), 1.0)
+    fill(V("pq", 0, 1), 1.0)
+    tt(V("r4"), X(V("iw2"), e1u), V("n2"), Op.max)
+    quant("qu", "su", 0, 128, "ut")
+    ts(V("r1"), V("r2"), col(7), Op.is_le, 1.0 / 4096, Op.mult)
+    cp((T.qr[:].bitcast(dt.uint32), "qr", np.arange(128)), X((T.qu[:].bitcast(dt.uint32), "qu", np.arange(128)), rep))
+    cp(V("sr"), X(V("su"), rep))
+    act(V("ops"), V("r1"), bias=-4.0, scale=col(8))
+    quant("qx0", "sx0", 0, C, "xt")
+    mm(4, "qr", "sr", 0, "qx0", "sx0", 0, C)
+    ts(V("d0"), V("r2"), col(7), Op.is_gt, 4.0, Op.mult)
+    tt(V("mm"), X(V("r1"), paru), V("r4"), Op.mult)
+    act(V("hold"), X(V("r3"), paru), Fn.Sign, scale=-1.0, bias=col(16))
+    at = 0
+    for c in range(K):
+        n = 16 * (c + 1)
+        act(V("junk", at, at + n), V("r5", 0, n), Fn.Sign, bias=V("cst", 2 * K + c, 2 * K + c + 1),
+            acc=V("cst", 14 * K + c, 14 * K + c + 1))
+        at += n
+    act(dum, nL, bias=float(SL))
+    act(n4, nL, scale=4.0, bias=6.0)
+    act(evn, nL, scale=4.0, bias=7.0)
+    act(nk, nL, scale=4.0)
+    act(col(14), col(12), scale=0.625)
+    for o, x in ((V("nn", 0, 32), 4.0), (V("nn", 32, 64), 6.0), (V("jj", 0, 1), 0.0), (V("bt", 2, 4), 0.0),
+                 (V("bt", SL - 2, SL), 0.0), (V("xp", C, 4 * PL, PL), 0.0), (V("yp", C, 4 * PL, PL), 0.0),
+                 (V("fo", 192, 4 * 208, 208), 0.0)):
+        act(o, V("ones", 0, len(o[2])), scale=x)
+    act(V("dm"), X(V("m16"), pmu))
+
+    def late_constants():
+        tt(V("d0"), V("d0"), V("mm"), Op.max)
+        ts(col(3), coli(6), 46.0, Op.mult)
+        ts(V("uu", 0, 16), V("ones", 0, 16), 0.0, Op.mult)
+        ts(V("uu", 368, 384), V("ones", 0, 16), 0.0, Op.mult)
+        ts(col(4), col(0), 2.0, Op.mult, col(3), Op.add)
+
+    def more_constants():
+        iota(V("vtb"), [[1, C], [512, 4]], 0, 0)
+        issue("g", lambda: g.affine_select(T.ew[:], T.ones[:], [[-1, 520]], Op.is_equal, 0.0, 3, 4), [V("ew")], [V("ones")])
+
+    def depths():
+        ts(dep, L("cst", 14), 0.5, Op.mult)
+        ts(pick, V("col", 24, 28), col(4), Op.add, 91.0, Op.min)
+        tt(dep, dep, koff, Op.add)
+        cp(depu, dep)
+        act(V("r2"), X(iw, depu))
+        act(V("td", 8, SL, 4), V("r2"), scale=-2.0, bias=-2.0)
+        act(V("td", 9, SL, 4), V("r2"), scale=-2.0, bias=-2.0)
+        act(V("c2t", 0, 4 * C, 4), V("r2"), scale=0.0, bias=-OFF)
+        act(V("c2t", 1, 4 * C, 4), V("r2"), bias=1.0 - OFF)
+        act(V("c2t", 2, 4 * C, 4), V("r2"), bias=2.0 - OFF)
+        act(V("c2t", 3, 4 * C, 4), V("r2"), scale=0.0, bias=-OFF)
+
+    def tables():
+        tt(V("bt", 6, SL - 2, 4), V("nf"), V("r2"), Op.subtract)
+        tt(V("pay"), X(iw, depu), V("nf"), Op.add)
+        act(V("bt", 7, SL - 1, 4), V("bt", 6, SL - 2, 4), bias=353.0 / 1024 - 1)
+        act(V("ga", C, 2 * C), V("oo"), scale=0.5, bias=0.5)
+
+    def defects(bank, a, b):
+        ts(V("bb", a, b), V("ps", 512 * bank, 512 * bank + b - a), 0.0, Op.is_gt, 0.5, Op.subtract)
+
+    def shifts(a, b):
+        tt(V("hh", a, b), V("bb", a, b), V("ops", a, b), Op.add)
+
+    def planes(t):
+        for b in range(4):
+            if t == 0:
+                act(V("xp", PL * b, PL * b + C), V("xt", b, 4 * C, 4))
+            else:
+                act(V("xp", PL * b, PL * b + C), V("tf", C * b, C * b + C), scale=0.0078125)
+
+    def layer(t, a, b, src, fbuf, fw, flist, olist, bank, meanwhile=None):
+        n, nf = b - a, 16 * len(flist[2])
+        for p in range(4):
+            act(V(fbuf, fw * p, fw * p + nf), X(V(src, PL * p, PL * p + C + 1), flist))
+        for p in range(4):
+            tt(V("zt", 4 * a + p, 4 * b, 4), X(V(src, PL * p, PL * p + C + 1), olist), V(fbuf, fw * p + 1, fw * p + 1 + n), Op.subtract)
+            act(V("z128", C * p + a, C * p + b), V("zt", 4 * a + p, 4 * b, 4), scale=128.0)
+        quant("qz", "zs", a, b, "zt")
+        for p in range(4):
+            mm(p, "qw", "sw", 128 * p, "qz", "zs", a, b)
+        if meanwhile:
+            meanwhile()
+        for p in range(4):
+            tt(V("tf", C * p + a, C * p + b), V("ps", 512 * p, 512 * p + n), V("z128", C * p + a, C * p + b), Op.add)
+            act(V("xt", 4 * a + p, 4 * b, 4), V("tf", C * p + a, C * p + b), scale=0.0078125)
+        qx, sx = "qx%d" % (t + 1), "sx%d" % (t + 1)
+        quant(qx, sx, a, b, "xt")
+        if t + 1 < R:
+            mm(bank, "qr", "sr", 0, qx, sx, a, b)
+            defects(bank, a, b)
+        else:
+            mm(bank, "qv", "sv", 0, qx, sx, a, b)
+            dma("s", T.oc[:, 4 * a:4 * b], T[qx][:, a:b].bitcast(dt.uint8), [], [V(qx, a, b)])
+            cp(V("yo", a, b), V("ps", 512 * bank, 512 * bank + n))
+            dma("s" if a else "a", T.y[:, a:b], T.yo[:, a:b], [], [V("yo", a, b)])
+
+    defects(4, 0, C)
+    for t in range(R):
+        dst = T.cores[(rank + STEP[t]) % N]
+        src = T.cores[(rank - STEP[t]) % N]
+        ne = len(topo.engines(src, core))
+        qx, sx, lq, ls, ll, lo = ("%s%d" % (k, t) for k in ("qx", "sx", "lq", "ls", "ll", "lo"))
+        send(dst, V(lq), V(qx), "big%d" % t, codes=True)
+        send(dst, V(ls), V(sx), "big%d" % t)
+        arrives("big%d" % t, 2 * ne, [V(lq), V(ls)])
+        arrives("lst%d" % t, ne, [V(ll)])
+        if t == 0:
+            more_constants()
+        else:
+            planes(t)
+
+        scan(V("pp", 1, C + 1), V("bb"), V("twos"), 1.0, Op.mult, Op.mult)
+        scan(V("pq", 1, C), V("bb", 0, C - 1), V("twos", 0, C - 1), 1.0, Op.mult, Op.mult)
+        shifts(0, A if t else C)
+        tt(V("oo"), X(V("pp", 0, C + 1), endu), V("pq", 0, C), Op.mult)
+        if t == 0:
+            late_constants()
+        tt(V("d1"), V("oo"), V("hh"), Op.add)
+        if t:
+            act(V("ga", C, 2 * C), V("oo"), scale=0.5, bias=0.5)
+        scan(V("vv"), V("d0"), V("d1"), 0.0, Op.min, Op.max)
+        scan(V("wd"), V("dmb"), V("d1"), 0.0, Op.add, Op.min)
+        tt(V("gg"), X(V("vv"), paru), V("mm"), Op.min)
+        if t == 0:
+            depths()
+        s = [L("sl", i) for i in range(24)]
+        kind, nbot, even, y, t5, m, rise, fall, br, bs, beg = s[:11]
+        tt(kind, diag("wd"), kthr, Op.subtract)
+        scan(V("uu", 16, 16 + C), V("hold"), V("gg"), 0.0, Op.mult, Op.max)
+        ts(nbot, kind, -0.5, Op.not_equal, 4096.0, Op.mult)
+        for o, i in ((V("tt", 0, C), V("uu", 16, 16 + C)), (V("tt", C, 736), V("uu"))):
+            issue("v", lambda: g.vector.transpose(o[0], i[0]), [o], [i])
+        ts(even, kind, 0.0, Op.is_gt, 4096.0, Op.mult)
+        scan(V("rr"), V("m8"), V("tt"), 0.0, Op.min, Op.max)
+        ts(V("r8", 0, 92), V("rr", 7, 736, 8), 4096.0, Op.mult)
+        tt(V("zi"), X(V("r8", 0, 92), pick), V("nn"), Op.max)
+        if t == 0:
+            tables()
+        e, t4, es = V("zi", 0, K), V("zi", 32, 32 + K), L("sli", 0)
+        ts(es, e, 2044, Op.bitwise_and)
+        tt(t5, t4, even, Op.add)
+        tt(y, e, nbot, Op.add)
+        tt(m, t5, es, Op.max)
+        tt(bs, t5, n4, Op.is_equal)
+        tt(L("lb", 0), y, dum, Op.min)
+        tt(br, y, m, Op.is_equal)
+        tt(L("lb", 2), m, evn, Op.min)
+        tt(beg, bs, br, Op.add)
+        tt(fall, e, m, Op.is_gt)
+        tt(s[11], beg, e, Op.mult)
+        tt(s[12], beg, br, Op.add)
+        tt(L("lb", 1), s[11], br, Op.add)
+        tt(s[12], s[12], even, Op.add)
+        cp(L("lu", 0, 3), L("lb", 0, 3))
+        tt(L("lb", 4), fall, e, Op.mult)
+        act(V("c1"), X(V("td"), L("lu", 1)), bias=OFF)
+        cp(X(V("bt"), L("lu", 0)), V("pay"))
+        act(V("gb"), X(V("bt", 0, SL), L("lu", 2)))
+        ts(s[12], s[12], 3.0, Op.min)
+        tt(V("ga", 0, C), X(V("bt", 0, SL), L("lu", 1)), V("c1"), Op.add)
+        tt(L("lb", 3), s[12], nk, Op.add)
+        tt(rise, e, m, Op.is_equal)
+        cp(L("lu", 3, 2), L("lb", 3, 2))
+        act(V("c2", 0, C), X(V("c2t"), L("lu", 3)))
+        act(V("c3"), X(V("td"), L("lu", 4)))
+        act(V("vr"), X(V("vtb"), L("lu", 3)))
+        ts(s[13], rise, -2.0, Op.mult, 1.0, Op.add)
+        scan(V("w"), V("dm"), V("gb"), 0.0, Op.add, Op.min)
+        tt(s[13], s[13], dep, Op.mult)
+        ts(L("sli", 1), diag("w"), col(12), Op.add, 1024.0, Op.mult)
+        tt(s[13], s[13], fall, Op.add)
+        ts(L("sli", 2), L("sli", 1), 1023, Op.bitwise_and)
+        ts(L("sli", 3), L("sli", 1), 10, Op.arith_shift_right)
+        cp(L("lu", 5), L("sli", 2))
+        tt(s[14], s[13], L("sli", 3), Op.add)
+        scan(V("jj", 1, 2 * C + 1), V("ga"), V("c2"), 0.0, Op.add, Op.add)
+        if t == 0:
+            act(V("dmh"), X(V("m16"), pmu), scale=0.625)
+            for b in range(4):
+                quant("qe", "se", 128 * b, 128 * b + 128, "ew", 3 - b)
+        tt(V("gf"), X(V("jj", 0, 2 * C + 1), L("lu", 5)), V("c3"), Op.add)
+        if t == 0:
+            planes(0)
+        for b in range(4):
+            mm(b, "qe", "se", 128 * b, lq, ls, 0, C)
+            act(V("yp", PL * b, PL * b + C), V("ps", 512 * b, 512 * b + C))
+        scan(V("wh"), V("dmh"), V("gf"), 0.0, Op.add, Op.min)
+        tt(s[15], diag("wh"), s[14], Op.add)
+        ts(L("lu", 6), s[15], col(14), Op.add)
+        cp(X(V("vo"), L("lu", 6)), V("vr"))
+        scan(V("w"), V("dm"), V("vo"), 0.0, Op.add, Op.min)
+        ts(L("sli", 1), diag("w"), col(12), Op.add)
+        ts(L(lo, 0), diag("w"), col(12), Op.add, float(C), Op.min)
+        ts(L("sli", 2), L("sli", 1), 511, Op.bitwise_and)
+        cp(L(lo, 1), L("sli", 2))
+        send(dst, V(ll), V(lo, 0, 32), "lst%d" % t)
+        layer(t, A, C, "xp", "fo", 208, V(lo, 10, K), V(lo, K + 10, 2 * K), 4,
+              (lambda: quant("qv", "sv", 0, 128, "vt")) if t == 0 else None)
+        if t + 1 == R:
+            act(V("otr"), X(iw, L(lo, 1)))
+            dma("s", T.ot[:], T.otr[0:128:16, :], [], [V("otr")])
+        layer(t, 0, A, "yp", "fl", 176, V(ll, 0, 11), V(ll, K, K + 10), 5, (lambda: shifts(A, C)) if t + 1 < R else None)
+
+    sx = "sx%d" % R
+    for k in range(4):
+        dma("sa"[k % 2], T.osc[4 * k:4 * k + 4, :], T[sx][32 * k:32 * k + 4, :], [], [V(sx)])
+    for sem, n in count.items():
+        g.wait_ge(T.sem[sem], n)

@@ -4,7 +4,7 @@ from concourse.mybir import dt, AluOpType as Op, AxisListType, ActivationFunctio
 C, A, R = 352, 160, 3
 STEP = [4, 2, 1]
 K = C // 16
-PL = 368
+PL = 720
 OFF = 12582912.0
 SL = 4 * C + 8
 BIG = 2048.0
@@ -16,16 +16,16 @@ _S = {
     "qv": (128, Q), "sv": (128, S8), "ew": (520, B16), "ones": (520, B16), "qe": (512, Q), "se": (512, S8),
     "qz": (C, Q), "zs": (C, S8), "zt": (4 * C, B16), "z128": (4 * C, B16), "tf": (4 * C, F),
     "xp": (4 * PL, B16), "yp": (4 * PL, B16), "fl": (4 * 176, B16), "fo": (4 * 208, B16),
-    "iot": (360, F), "iw2": (708, F), "m16": (16, F), "dm": (C, F), "dmb": (C, B16), "dmh": (C, B16),
+    "iot": (360, F), "iw2": (708, F), "io2": (708, F), "m16": (16, F), "dm": (C, F), "dmb": (C, B16), "dmh": (C, B16),
     "m8": (736, B16), "twos": (C, B16), "nn": (64, F),
     "col": (32, F), "coli": (16, I), "cst": (16 * K, F), "csti": (K, I), "su16": (8 * K, U16),
-    "r1": (C, F), "r2": (C, F), "r3": (C, F), "r4": (C, F), "r5": (C, F), "n2": (C, F), "nf": (C, F),
+    "r1": (C, F), "r2": (C, F), "r3": (C, F), "r4": (C, F), "r5": (C, F), "r6": (C, F), "n2": (C, F), "nf": (C, F),
     "mm": (C, H16), "d0": (C, H16), "hold": (C, B16), "ops": (C, B16), "junk": (4048, B16),
     "pay": (C, F), "bt": (SL + C, F), "td": (SL, F), "c2t": (4 * C, F), "vtb": (4 * C, F),
-    "bb": (C, B16), "hh": (C, B16), "pp": (PL, B16), "pq": (PL, B16), "oo": (C, B16), "d1": (C, B16), "vv": (C, F),
-    "gg": (C, H16), "uu": (384, H16), "tt": (736, H16), "rr": (736, H16), "r8": (96, F), "zi": (64, I),
+    "bb": (C, B16), "hh": (C, B16), "pp": (368, B16), "pq": (368, B16), "oo": (C, B16), "d1": (C, B16), "vv": (C, F),
+    "ee": (C, F), "gg": (C, H16), "uu": (384, H16), "tt": (736, H16), "rr": (736, H16), "r8": (96, F), "zi": (64, I),
     "wd": (C, B16), "sl": (24 * K, F), "sli": (4 * K, I), "lb": (5 * K, F), "lu": (8 * K, U16),
-    "c1": (C, F), "c3": (C, F), "gb": (C, F), "vr": (C, F), "ga": (2 * C, F), "c2": (2 * C, F), "jj": (712, F),
+    "c1": (C, F), "c3": (C, F), "gb": (C, F), "vr": (C, F), "ga": (C, F), "c2": (C, F), "jj": (712, F),
     "gf": (C, H16), "wh": (C, H16), "w": (C, F), "vo": (C, F), "otr": (C, F), "yo": (C, F),
 }
 for _t in range(R + 1):
@@ -38,7 +38,7 @@ for _t in range(R):
     _S["lo%d" % _t] = (2 * K, U16)
 SCRATCH = {k: ("sbuf", [128, n], d) for k, (n, d) in _S.items()}
 SCRATCH["ps"] = ("psum", [128, 4096], "float32")
-NDMA = 20
+NDMA = 44
 SEMAPHORES = (["cv", "ca", "ct", "cg", "sent"] + ["dma%d" % i for i in range(NDMA)]
               + ["big%d" % t for t in range(R)] + ["lst%d" % t for t in range(R)])
 
@@ -201,7 +201,6 @@ def rank_program(g, core, T, topo):
     iota(V("col", 24, 28), [[1, 2], [32, 2]], 0, 0)
     iota(V("m8"), [[0, 92], [1, 8]], 0, 0)
     iota(V("td"), [[0, SL]], 0, 0)
-    iota(V("c2", C, 2 * C), [[0, C]], 0, 0)
     fill(V("ones"), 1.0)
     fill(V("twos"), -2.0)
     act(V("bt", 0, SL, 4), V("ones", 0, 354), scale=0.0)
@@ -218,60 +217,59 @@ def rank_program(g, core, T, topo):
     nbias, dum, n4, evn, koff, kthr, nk, dep = (L("cst", i) for i in (2, 3, 4, 5, 6, 7, 8, 9))
     szu, paru, endu, e1u, depu, pmu = (L("su16", i) for i in range(6))
     pick, rep = V("su16", 6 * K, 6 * K + 4), V("su16", 7 * K, 7 * K + 8)
+    fill(V("pp", 0, 1), 1.0)
+    fill(V("pq", 0, 1), 1.0)
+    ts(V("r8", 16, 24), V("m16", 0, 8), col(1), Op.is_equal)
     ts(nL, L("cst", 0), col(0), Op.add)
     ts(col(9), col(2), -2.0, Op.mult, 5.0, Op.add)
     ts(col(10), col(2), 4.0, Op.mult)
-    ts(col(11), col(2), 6.0, Op.mult)
-    ts(col(12), col(0), 15.0, Op.is_lt, BIG, Op.mult)
-    ts(coli(6), coli(5), 1, Op.bitwise_and)
-    ts(pmu, L("cst", 0), 0.0, Op.mult, col(0), Op.add)
-    cp(rep, V("cst", 0, 8))
-    ts(V("r8", 16, 24), V("m16", 0, 8), col(1), Op.is_equal)
-    ts(V("r8", 32, 48), V("m16"), col(0), Op.subtract)
-    act(V("n2"), V("iot", 0, C), scale=col(10), bias=col(11))
-    act(nbias, nL, scale=-1.0, bias=-0.5)
-    ts(col(15), col(0), 0.5, Op.mult, -8.0, Op.add)
     tt(V("r8", 24, 32), V("r8", 0, 8), V("r8", 16, 24), Op.mult)
+    ts(col(11), col(2), 6.0, Op.mult)
+    ts(V("r8", 32, 48), V("m16"), col(0), Op.subtract)
+    ts(pmu, L("cst", 0), 0.0, Op.mult, col(0), Op.add)
+    issue("v", lambda: g.vector.tensor_reduce(col(5)[0], V("r8", 24, 32)[0], AxisListType.X, Op.add), [col(5)], [V("r8", 24, 32)])
     ts(V("r8", 48, 64), V("r8", 32, 48), 0.0, Op.is_equal, 4 * BIG, Op.mult)
     ts(V("r8", 64, 80), V("r8", 32, 48), 1.0, Op.is_equal, -BIG, Op.mult)
-    ts(col(8), col(9), 4096.0, Op.mult)
-    issue("v", lambda: g.vector.tensor_reduce(col(5)[0], V("r8", 24, 32)[0], AxisListType.X, Op.add), [col(5)], [V("r8", 24, 32)])
-    tt(V("m16"), V("r8", 48, 64), V("r8", 64, 80), Op.add)
-    ts(col(13), col(12), -1.0 / 64, Op.mult, -4.0, Op.add)
+    act(V("n2"), V("iot", 0, C), scale=col(10), bias=col(11))
+    act(nbias, nL, scale=-1.0, bias=-0.5)
+    ts(col(12), col(0), 15.0, Op.is_lt, BIG, Op.mult)
     ts(col(6), col(5), -1.5, Op.mult)
+    tt(V("m16"), V("r8", 48, 64), V("r8", 64, 80), Op.add)
+    ts(col(15), col(0), 0.5, Op.mult, -8.0, Op.add)
+    cp(rep, V("cst", 0, 8))
     ts(col(7), col(5), 0.5, Op.mult)
-    ts(col(16), col(5), -0.5, Op.add)
+    act(col(8), col(9), scale=4096.0)
+    act(col(13), col(12), scale=-1.0 / 64, bias=-4.0)
+    act(col(16), col(5), bias=-0.5)
+    act(col(18), col(5), scale=-4.0)
     act(koff, nL, scale=0.5, bias=col(15))
-    act(V("nf"), V("iot", 0, C), scale=1.0 / 1024)
     act(V("dmb"), X(V("m16"), pmu), scale=1.0 / 64)
 
     cp(szu, V("szi"))
     tt(V("csti"), V("szi"), nL, Op.add)
-    cp(paru, V("pri"))
     ts(L("cst", 10), V("pri"), 1.0, Op.add)
     ts(L("cst", 11), V("pri"), 2.0, Op.mult, 4.0, Op.add)
-    cp(endu, V("csti"))
+    cp(paru, V("pri"))
     act(V("r2"), X(iw, szu), Fn.Abs, bias=col(6))
     act(V("r3"), X(iw, szu))
-    act(V("r5"), X(iw, endu))
     tt(L("cst", 10), L("cst", 10), nL, Op.not_equal)
+    cp(endu, V("csti"))
+    act(V("r5"), X(iw, endu))
     ts(L("cst", 12), V("szi"), col(5), Op.is_ge, col(9), Op.mult)
-    ts(L("cst", 13), V("szi"), 0.5, Op.mult, col(5), Op.is_le)
     tt(L("cst", 11), L("cst", 11), L("cst", 10), Op.add)
-    tt(L("cst", 12), L("cst", 12), L("cst", 13), Op.mult)
+    ts(L("cst", 13), V("szi"), 0.5, Op.mult, col(5), Op.is_le)
+    ts(coli(6), coli(5), 1, Op.bitwise_and)
     cp(e1u, L("cst", 11))
-    ts(kthr, L("cst", 12), col(13), Op.add)
-    fill(V("pp", 0, 1), 1.0)
-    fill(V("pq", 0, 1), 1.0)
-    tt(V("r4"), X(V("iw2"), e1u), V("n2"), Op.max)
+    tt(L("cst", 12), L("cst", 12), L("cst", 13), Op.mult)
     quant("qu", "su", 0, 128, "ut")
-    ts(V("r1"), V("r2"), col(7), Op.is_le, 1.0 / 4096, Op.mult)
+    tt(V("r4"), X(V("iw2"), e1u), V("n2"), Op.max)
     cp((T.qr[:].bitcast(dt.uint32), "qr", np.arange(128)), X((T.qu[:].bitcast(dt.uint32), "qu", np.arange(128)), rep))
     cp(V("sr"), X(V("su"), rep))
-    act(V("ops"), V("r1"), bias=-4.0, scale=col(8))
+    ts(V("r1"), V("r2"), col(7), Op.is_le, 1.0 / 4096, Op.mult)
     quant("qx0", "sx0", 0, C, "xt")
+    act(V("ops"), V("r1"), bias=-4.0, scale=col(8))
+    act(V("r6"), V("r2"), Fn.Relu, scale=8.0, bias=col(18))
     mm(4, "qr", "sr", 0, "qx0", "sx0", 0, C)
-    ts(V("d0"), V("r2"), col(7), Op.is_gt, 4.0, Op.mult)
     tt(V("mm"), X(V("r1"), paru), V("r4"), Op.mult)
     act(V("hold"), X(V("r3"), paru), Fn.Sign, scale=-1.0, bias=col(16))
     at = 0
@@ -289,25 +287,17 @@ def rank_program(g, core, T, topo):
                  (V("bt", SL - 2, SL), 0.0), (V("xp", C, 4 * PL, PL), 0.0), (V("yp", C, 4 * PL, PL), 0.0),
                  (V("fo", 192, 4 * 208, 208), 0.0)):
         act(o, V("ones", 0, len(o[2])), scale=x)
-    act(V("dm"), X(V("m16"), pmu))
-
-    def late_constants():
-        tt(V("d0"), V("d0"), V("mm"), Op.max)
-        ts(col(3), coli(6), 46.0, Op.mult)
-        ts(V("uu", 0, 16), V("ones", 0, 16), 0.0, Op.mult)
-        ts(V("uu", 368, 384), V("ones", 0, 16), 0.0, Op.mult)
-        ts(col(4), col(0), 2.0, Op.mult, col(3), Op.add)
+    act(V("nf"), V("iot", 0, C), scale=1.0 / 1024)
 
     def more_constants():
-        iota(V("vtb"), [[1, C], [512, 4]], 0, 0)
+        iota(V("vtb"), [[1, C], [0, 4]], C + 1, 0)
+        iota(V("vtb", 0, 4 * C, 4), [[1, C]], 0, 0)
         issue("g", lambda: g.affine_select(T.ew[:], T.ones[:], [[-1, 520]], Op.is_equal, 0.0, 3, 4), [V("ew")], [V("ones")])
+        iota(V("io2", 0, 706), [[0, 2], [1, C + 1]], 0, 0)
 
-    def depths():
-        ts(dep, L("cst", 14), 0.5, Op.mult)
-        ts(pick, V("col", 24, 28), col(4), Op.add, 91.0, Op.min)
-        tt(dep, dep, koff, Op.add)
-        cp(depu, dep)
+    def depth_tables():
         act(V("r2"), X(iw, depu))
+        act(V("dm"), X(V("m16"), pmu))
         act(V("td", 8, SL, 4), V("r2"), scale=-2.0, bias=-2.0)
         act(V("td", 9, SL, 4), V("r2"), scale=-2.0, bias=-2.0)
         act(V("c2t", 0, 4 * C, 4), V("r2"), scale=0.0, bias=-OFF)
@@ -315,52 +305,62 @@ def rank_program(g, core, T, topo):
         act(V("c2t", 2, 4 * C, 4), V("r2"), bias=2.0 - OFF)
         act(V("c2t", 3, 4 * C, 4), V("r2"), scale=0.0, bias=-OFF)
 
-    def tables():
-        tt(V("bt", 6, SL - 2, 4), V("nf"), V("r2"), Op.subtract)
-        tt(V("pay"), X(iw, depu), V("nf"), Op.add)
-        act(V("bt", 7, SL - 1, 4), V("bt", 6, SL - 2, 4), bias=353.0 / 1024 - 1)
-        act(V("ga", C, 2 * C), V("oo"), scale=0.5, bias=0.5)
-
     def defects(bank, a, b):
         ts(V("bb", a, b), V("ps", 512 * bank, 512 * bank + b - a), 0.0, Op.is_gt, 0.5, Op.subtract)
 
     def shifts(a, b):
         tt(V("hh", a, b), V("bb", a, b), V("ops", a, b), Op.add)
 
-    def planes(t):
-        for b in range(4):
-            if t == 0:
-                act(V("xp", PL * b, PL * b + C), V("xt", b, 4 * C, 4))
-            else:
-                act(V("xp", PL * b, PL * b + C), V("tf", C * b, C * b + C), scale=0.0078125)
+    def plane(name, b, src):
+        o, i = V(name, PL * b + C + 1, PL * b + 2 * C + 1), V(name, PL * b, PL * b + C)
+        act(i, src)
+        dma("s", o[0], i[0], [o], [i])
 
-    def layer(t, a, b, src, fbuf, fw, flist, olist, bank, meanwhile=None):
+    def xplane(b):
+        plane("xp", b, V("xt", b, 4 * C, 4))
+
+    def result(a, b, bank):
+        cp(V("yo", a, b), V("ps", 512 * bank, 512 * bank + b - a))
+        dma("s" if a else "a", T.y[:, a:b], T.yo[:, a:b], [], [V("yo", a, b)])
+
+    def layer(t, a, b, src, fbuf, fw, flist, olist, bank, first=None, meanwhile=None):
         n, nf = b - a, 16 * len(flist[2])
         for p in range(4):
             act(V(fbuf, fw * p, fw * p + nf), X(V(src, PL * p, PL * p + C + 1), flist))
         for p in range(4):
-            tt(V("zt", 4 * a + p, 4 * b, 4), X(V(src, PL * p, PL * p + C + 1), olist), V(fbuf, fw * p + 1, fw * p + 1 + n), Op.subtract)
-            act(V("z128", C * p + a, C * p + b), V("zt", 4 * a + p, 4 * b, 4), scale=128.0)
+            tt(V("zt", 4 * a + p, 4 * b, 4), X(V(src, PL * p, PL * p + 2 * C + 1), olist), V(fbuf, fw * p + 1, fw * p + 1 + n), Op.subtract)
+            if p < 3:
+                act(V("z128", C * p + a, C * p + b), V("zt", 4 * a + p, 4 * b, 4), scale=128.0)
+            if p == 1 and first:
+                first()
         quant("qz", "zs", a, b, "zt")
-        for p in range(4):
+        for p in (3, 0, 1, 2):
             mm(p, "qw", "sw", 128 * p, "qz", "zs", a, b)
+        act(V("tf", 3 * C + a, 3 * C + b), V("ps", 1536, 1536 + n), scale=0.0078125)
         if meanwhile:
             meanwhile()
-        for p in range(4):
+        for p in range(3):
             tt(V("tf", C * p + a, C * p + b), V("ps", 512 * p, 512 * p + n), V("z128", C * p + a, C * p + b), Op.add)
             act(V("xt", 4 * a + p, 4 * b, 4), V("tf", C * p + a, C * p + b), scale=0.0078125)
+        tt(V("xt", 4 * a + 3, 4 * b, 4), V("tf", 3 * C + a, 3 * C + b), V("zt", 4 * a + 3, 4 * b, 4), Op.add)
         qx, sx = "qx%d" % (t + 1), "sx%d" % (t + 1)
         quant(qx, sx, a, b, "xt")
         if t + 1 < R:
             mm(bank, "qr", "sr", 0, qx, sx, a, b)
-            defects(bank, a, b)
         else:
             mm(bank, "qv", "sv", 0, qx, sx, a, b)
             dma("s", T.oc[:, 4 * a:4 * b], T[qx][:, a:b].bitcast(dt.uint8), [], [V(qx, a, b)])
-            cp(V("yo", a, b), V("ps", 512 * bank, 512 * bank + n))
-            dma("s" if a else "a", T.y[:, a:b], T.yo[:, a:b], [], [V("yo", a, b)])
+
+    def evens(i):
+        a, b = 88 * i, 88 * i + 88
+        scan(V("ee", a, b), V("oo", a, b), V("ones", a, b), V("ee", a - 1, a) if i else 0.0, Op.add, Op.add)
+        if i == 3:
+            act(col(17), V("ee", C - 1, C), scale=-0.5, bias=float(C))
+            act(V("jj", C + 1, 2 * C + 1), V("ee"), scale=0.5, bias=col(17))
 
     defects(4, 0, C)
+    ts(kthr, L("cst", 12), col(13), Op.add)
+    ts(col(3), coli(6), 46.0, Op.mult)
     for t in range(R):
         dst = T.cores[(rank + STEP[t]) % N]
         src = T.cores[(rank - STEP[t]) % N]
@@ -373,102 +373,136 @@ def rank_program(g, core, T, topo):
         if t == 0:
             more_constants()
         else:
-            planes(t)
+            for b in range(4):
+                xplane(b)
 
         scan(V("pp", 1, C + 1), V("bb"), V("twos"), 1.0, Op.mult, Op.mult)
         scan(V("pq", 1, C), V("bb", 0, C - 1), V("twos", 0, C - 1), 1.0, Op.mult, Op.mult)
-        shifts(0, A if t else C)
+        if t == 0:
+            shifts(0, C)
         tt(V("oo"), X(V("pp", 0, C + 1), endu), V("pq", 0, C), Op.mult)
         if t == 0:
-            late_constants()
+            tt(V("d0"), V("r6"), V("mm"), Op.max)
+        else:
+            shifts(0, A)
         tt(V("d1"), V("oo"), V("hh"), Op.add)
-        if t:
-            act(V("ga", C, 2 * C), V("oo"), scale=0.5, bias=0.5)
+        evens(0)
+        if t == 0:
+            ts(col(4), col(0), 2.0, Op.mult, col(3), Op.add)
         scan(V("vv"), V("d0"), V("d1"), 0.0, Op.min, Op.max)
         scan(V("wd"), V("dmb"), V("d1"), 0.0, Op.add, Op.min)
         tt(V("gg"), X(V("vv"), paru), V("mm"), Op.min)
-        if t == 0:
-            depths()
         s = [L("sl", i) for i in range(24)]
-        kind, nbot, even, y, t5, m, rise, fall, br, bs, beg = s[:11]
+        kind, nbot, even, y, t5, m, rise, fall, br, bs = s[:10]
         tt(kind, diag("wd"), kthr, Op.subtract)
+        if t == 0:
+            xplane(0)
+            ts(dep, L("cst", 14), 0.5, Op.mult)
+            ts(V("uu", 0, 16), V("ones", 0, 16), 0.0, Op.mult)
+            ts(V("uu", 368, 384), V("ones", 0, 16), 0.0, Op.mult)
+        evens(1)
+        if t == 0:
+            tt(dep, dep, koff, Op.add)
         scan(V("uu", 16, 16 + C), V("hold"), V("gg"), 0.0, Op.mult, Op.max)
+        if t == 0:
+            cp(depu, dep)
+            depth_tables()
         ts(nbot, kind, -0.5, Op.not_equal, 4096.0, Op.mult)
+        ts(even, kind, 0.0, Op.is_gt, 4096.0, Op.mult)
         for o, i in ((V("tt", 0, C), V("uu", 16, 16 + C)), (V("tt", C, 736), V("uu"))):
             issue("v", lambda: g.vector.transpose(o[0], i[0]), [o], [i])
-        ts(even, kind, 0.0, Op.is_gt, 4096.0, Op.mult)
+        evens(2)
+        if t == 0:
+            ts(pick, V("col", 24, 28), col(4), Op.add, 91.0, Op.min)
         scan(V("rr"), V("m8"), V("tt"), 0.0, Op.min, Op.max)
+        evens(3)
+        ts(s[16], even, 3.0, Op.min)
         ts(V("r8", 0, 92), V("rr", 7, 736, 8), 4096.0, Op.mult)
+        if t == 0:
+            tt(V("pay"), X(iw, depu), V("nf"), Op.add)
+        tt(s[16], s[16], nk, Op.add)
         tt(V("zi"), X(V("r8", 0, 92), pick), V("nn"), Op.max)
         if t == 0:
-            tables()
+            tt(V("bt", 6, SL - 2, 4), V("nf"), V("r2"), Op.subtract)
+            act(V("bt", 7, SL - 1, 4), V("bt", 6, SL - 2, 4), bias=353.0 / 1024 - 1)
+            xplane(1)
         e, t4, es = V("zi", 0, K), V("zi", 32, 32 + K), L("sli", 0)
         ts(es, e, 2044, Op.bitwise_and)
         tt(t5, t4, even, Op.add)
         tt(y, e, nbot, Op.add)
+        ts(s[17], e, 1.0, Op.add)
         tt(m, t5, es, Op.max)
         tt(bs, t5, n4, Op.is_equal)
         tt(L("lb", 0), y, dum, Op.min)
         tt(br, y, m, Op.is_equal)
+        tt(s[11], bs, e, Op.mult)
         tt(L("lb", 2), m, evn, Op.min)
-        tt(beg, bs, br, Op.add)
+        tt(s[12], br, s[17], Op.mult)
         tt(fall, e, m, Op.is_gt)
-        tt(s[11], beg, e, Op.mult)
-        tt(s[12], beg, br, Op.add)
-        tt(L("lb", 1), s[11], br, Op.add)
-        tt(s[12], s[12], even, Op.add)
+        tt(s[16], s[16], bs, Op.add)
+        tt(L("lb", 1), s[11], s[12], Op.max)
+        ts(s[18], br, 2.0, Op.mult)
+        tt(rise, e, m, Op.is_equal)
         cp(L("lu", 0, 3), L("lb", 0, 3))
         tt(L("lb", 4), fall, e, Op.mult)
+        tt(L("lb", 3), s[16], s[18], Op.add)
         act(V("c1"), X(V("td"), L("lu", 1)), bias=OFF)
+        if t == 0:
+            xplane(2)
+            xplane(3)
         cp(X(V("bt"), L("lu", 0)), V("pay"))
         act(V("gb"), X(V("bt", 0, SL), L("lu", 2)))
-        ts(s[12], s[12], 3.0, Op.min)
-        tt(V("ga", 0, C), X(V("bt", 0, SL), L("lu", 1)), V("c1"), Op.add)
-        tt(L("lb", 3), s[12], nk, Op.add)
-        tt(rise, e, m, Op.is_equal)
         cp(L("lu", 3, 2), L("lb", 3, 2))
-        act(V("c2", 0, C), X(V("c2t"), L("lu", 3)))
+        ts(s[13], rise, -2.0, Op.mult, 1.0, Op.add)
+        tt(V("ga"), X(V("bt", 0, SL), L("lu", 1)), V("c1"), Op.add)
+        act(V("c2"), X(V("c2t"), L("lu", 3)))
         act(V("c3"), X(V("td"), L("lu", 4)))
         act(V("vr"), X(V("vtb"), L("lu", 3)))
-        ts(s[13], rise, -2.0, Op.mult, 1.0, Op.add)
-        scan(V("w"), V("dm"), V("gb"), 0.0, Op.add, Op.min)
         tt(s[13], s[13], dep, Op.mult)
-        ts(L("sli", 1), diag("w"), col(12), Op.add, 1024.0, Op.mult)
+        scan(V("w"), V("dm"), V("gb"), 0.0, Op.add, Op.min)
         tt(s[13], s[13], fall, Op.add)
+        if t == 0:
+            quant("qe", "se", 0, 128, "ew", 3)
+        ts(L("sli", 1), diag("w"), col(12), Op.add, 1024.0, Op.mult)
+        scan(V("jj", 1, 177), V("ga", 0, 176), V("c2", 0, 176), 0.0, Op.add, Op.add)
         ts(L("sli", 2), L("sli", 1), 1023, Op.bitwise_and)
         ts(L("sli", 3), L("sli", 1), 10, Op.arith_shift_right)
+        scan(V("jj", 177, C + 1), V("ga", 176, C), V("c2", 176, C), V("jj", 176, 177), Op.add, Op.add)
         cp(L("lu", 5), L("sli", 2))
         tt(s[14], s[13], L("sli", 3), Op.add)
-        scan(V("jj", 1, 2 * C + 1), V("ga"), V("c2"), 0.0, Op.add, Op.add)
         if t == 0:
             act(V("dmh"), X(V("m16"), pmu), scale=0.625)
-            for b in range(4):
-                quant("qe", "se", 128 * b, 128 * b + 128, "ew", 3 - b)
+            quant("qe", "se", 128, 256, "ew", 2)
         tt(V("gf"), X(V("jj", 0, 2 * C + 1), L("lu", 5)), V("c3"), Op.add)
         if t == 0:
-            planes(0)
+            quant("qe", "se", 256, 384, "ew", 1)
+        scan(V("wh"), V("dmh"), V("gf"), 0.0, Op.add, Op.min)
+        if t == 0:
+            quant("qe", "se", 384, 512, "ew", 0)
         for b in range(4):
             mm(b, "qe", "se", 128 * b, lq, ls, 0, C)
-            act(V("yp", PL * b, PL * b + C), V("ps", 512 * b, 512 * b + C))
-        scan(V("wh"), V("dmh"), V("gf"), 0.0, Op.add, Op.min)
+            plane("yp", b, V("ps", 512 * b, 512 * b + C))
         tt(s[15], diag("wh"), s[14], Op.add)
+        if t == 0:
+            quant("qv", "sv", 0, 128, "vt")
         ts(L("lu", 6), s[15], col(14), Op.add)
         cp(X(V("vo"), L("lu", 6)), V("vr"))
         scan(V("w"), V("dm"), V("vo"), 0.0, Op.add, Op.min)
-        ts(L("sli", 1), diag("w"), col(12), Op.add)
         ts(L(lo, 0), diag("w"), col(12), Op.add, float(C), Op.min)
-        ts(L("sli", 2), L("sli", 1), 511, Op.bitwise_and)
-        cp(L(lo, 1), L("sli", 2))
+        ts(L(lo, 1), diag("w"), col(12), Op.add)
         send(dst, V(ll), V(lo, 0, 32), "lst%d" % t)
-        layer(t, A, C, "xp", "fo", 208, V(lo, 10, K), V(lo, K + 10, 2 * K), 4,
-              (lambda: quant("qv", "sv", 0, 128, "vt")) if t == 0 else None)
-        if t + 1 == R:
-            act(V("otr"), X(iw, L(lo, 1)))
+        layer(t, A, C, "xp", "fo", 208, V(lo, 10, K), V(lo, K + 10, 2 * K), 4)
+        if t + 1 < R:
+            layer(t, 0, A, "yp", "fl", 176, V(ll, 0, 11), V(ll, K, K + 10), 5, lambda: defects(4, A, C), lambda: shifts(A, C))
+            defects(5, 0, A)
+        else:
+            layer(t, 0, A, "yp", "fl", 176, V(ll, 0, 11), V(ll, K, K + 10), 5, None, lambda: result(A, C, 4))
+            act(V("otr"), X(V("io2", 0, 706), L(lo, 1)))
             dma("s", T.ot[:], T.otr[0:128:16, :], [], [V("otr")])
-        layer(t, 0, A, "yp", "fl", 176, V(ll, 0, 11), V(ll, K, K + 10), 5, (lambda: shifts(A, C)) if t + 1 < R else None)
+            sx = "sx%d" % R
+            for k in range(4):
+                dma("sa"[k % 2], T.osc[4 * k:4 * k + 4, :], T[sx][32 * k:32 * k + 4, :], [], [V(sx)])
+            result(0, A, 5)
 
-    sx = "sx%d" % R
-    for k in range(4):
-        dma("sa"[k % 2], T.osc[4 * k:4 * k + 4, :], T[sx][32 * k:32 * k + 4, :], [], [V(sx)])
     for sem, n in count.items():
         g.wait_ge(T.sem[sem], n)

import numpy as np
from concourse.mybir import dt, AluOpType as Op, AxisListType, ActivationFunctionType as Fn

C, A, R = 352, 160, 3
STEP = [4, 2, 1]
K = C // 16
PL = 720
OFF = 12582912.0
SL = 4 * C + 8
BIG = 2048.0
F, B16, H16, I, U16, Q, S8 = "float32", "bfloat16", "float16", "int32", "uint16", "float8_e4m3fn_x4", "uint8"

_S = {
    "szi": (K, I), "pri": (K, I), "xt": (4 * C, B16), "ut": (512, B16), "vt": (512, B16),
    "qw": (512, Q), "sw": (512, S8), "qu": (128, Q), "su": (128, S8), "qr": (128, Q), "sr": (128, S8),
    "qv": (128, Q), "sv": (128, S8), "ew": (520, B16), "ones": (520, B16), "qe": (512, Q), "se": (512, S8),
    "qz": (C, Q), "zs": (C, S8), "zt": (4 * C, B16), "z128": (4 * C, B16), "tf": (4 * C, F),
    "xp": (4 * PL, B16), "yp": (4 * PL, B16), "fl": (4 * 176, B16), "fo": (4 * 208, B16),
    "iot": (360, F), "iw2": (708, F), "io2": (708, F), "m16": (16, F), "dm": (C, F), "dmb": (C, B16), "dmh": (C, B16),
    "m8": (736, B16), "twos": (C, B16), "nn": (64, F),
    "col": (32, F), "coli": (16, I), "cst": (16 * K, F), "csti": (K, I), "su16": (8 * K, U16),
    "r1": (C, F), "r2": (C, F), "r3": (C, F), "r4": (C, F), "r5": (C, F), "r6": (C, F), "n2": (C, F), "nf": (C, F),
    "mm": (C, H16), "d0": (C, H16), "hold": (C, B16), "ops": (C, B16), "junk": (4048, B16),
    "pay": (C, F), "bt": (SL + C, F), "td": (SL, F), "c2t": (4 * C, F), "vtb": (4 * C, F),
    "bb": (C, B16), "hh": (C, B16), "pp": (368, B16), "pq": (368, B16), "oo": (C, B16), "d1": (C, B16), "vv": (C, F),
    "ee": (C, F), "gg": (C, H16), "uu": (384, H16), "tt": (736, H16), "rr": (736, H16), "r8": (96, F), "zi": (64, I),
    "wd": (C, B16), "sl": (24 * K, F), "sli": (4 * K, I), "lb": (5 * K, F), "lu": (8 * K, U16),
    "c1": (C, F), "c3": (C, F), "gb": (C, F), "vr": (C, F), "ga": (C, F), "c2": (C, F), "jj": (712, F),
    "gf": (C, H16), "wh": (C, H16), "w": (C, F), "vo": (C, F), "otr": (C, F), "yo": (C, F),
}
for _t in range(R + 1):
    _S["qx%d" % _t] = (C, Q)
    _S["sx%d" % _t] = (C, S8)
for _t in range(R):
    _S["lq%d" % _t] = (C, Q)
    _S["ls%d" % _t] = (C, S8)
    _S["ll%d" % _t] = (32, U16)
    _S["lo%d" % _t] = (2 * K, U16)
SCRATCH = {k: ("sbuf", [128, n], d) for k, (n, d) in _S.items()}
SCRATCH["ps"] = ("psum", [128, 4096], "float32")
NDMA = 44
SEMAPHORES = (["cv", "ca", "ct", "cg", "sent"] + ["dma%d" % i for i in range(NDMA)]
              + ["big%d" % t for t in range(R)] + ["lst%d" % t for t in range(R)])


def rank_program(g, core, T, topo):
    rank = T.rank_of(core)
    if rank is None:
        return
    N = len(T.cores)
    eng = {"v": g.vector, "a": g.scalar, "t": g.tensor, "g": g, "s": g.sync}
    own = {"v": "cv", "a": "ca", "t": "ct", "g": "cg"}
    count = {}
    clock = {q: {} for q in eng}
    events = [None]
    width = {k: v[1][1] for k, v in SCRATCH.items()}
    width["ps"] = 8
    wr = {k: np.zeros(n, np.int64) for k, n in width.items()}
    rd = {k: {} for k in width}
    ndma = [0]

    def V(name, a=0, b=None, s=1):
        b = SCRATCH[name][1][1] if b is None else b
        ap = T[name][:, a:b] if s == 1 else T[name][:, a:b:s]
        if name == "ps":
            return (ap, name, np.arange(a // 512, (b - 1) // 512 + 1))
        return (ap, name, np.arange(a, b, s))

    def X(win, off):
        return (win[0].indirect(off[0]), win[1], win[2], off)

    def wait(q, e):
        sem, val, seen = events[e]
        if clock[q].get(sem, 0) < val:
            eng[q].wait_ge(T.sem[sem], val)
            clock[q][sem] = val
        for k, x in seen.items():
            if clock[q].get(k, 0) < x:
                clock[q][k] = x

    def issue(q, call, outs, ins, sem=None, inc=1, direct=False):
        reads, writes = [], []
        for v in ins:
            if isinstance(v, tuple):
                (writes if v[1] == "ps" else reads).append(v)
                if len(v) == 4:
                    reads.append(v[3])
        for v in outs:
            writes.append(v)
            if len(v) == 4:
                reads.append(v[3])
        need = set()
        for v in reads + writes:
            need.update(np.unique(wr[v[1]][v[2]]).tolist())
        for v in writes:
            for arr in rd[v[1]].values():
                need.update(np.unique(arr[v[2]]).tolist())
        need.discard(0)
        for e in sorted(need, reverse=True):
            wait(q, e)
        sem = own[q] if sem is None else sem
        made = call()
        if not direct:
            made.then_inc(T.sem[sem], inc)
        count[sem] = count.get(sem, 0) + inc
        events.append((sem, count[sem], dict(clock[q])))
        e = len(events) - 1
        for v in reads:
            if sem not in rd[v[1]]:
                rd[v[1]][sem] = np.zeros(width[v[1]], np.int64)
            rd[v[1]][sem][v[2]] = e
        for v in writes:
            wr[v[1]][v[2]] = e

    def ap(x):
        return x[0] if isinstance(x, tuple) else x

    def cp(o, i):
        issue("v", lambda: g.vector.tensor_copy(o[0], i[0]), [o], [i])

    def tt(o, a, b, op):
        issue("v", lambda: g.vector.tensor_tensor(o[0], a[0], b[0], op), [o], [a, b])

    def ts(o, a, s1, op0, s2=None, op1=None):
        if op1 is None:
            issue("v", lambda: g.vector.tensor_scalar(o[0], a[0], ap(s1), None, op0), [o], [a, s1])
        else:
            issue("v", lambda: g.vector.tensor_scalar(o[0], a[0], ap(s1), ap(s2), op0, op1), [o], [a, s1, s2])

    def scan(o, a, b, init, op0, op1):
        issue("v", lambda: g.vector.tensor_tensor_scan(o[0], a[0], b[0], ap(init), op0, op1), [o], [a, b, init])

    def fill(o, x):
        issue("v", lambda: g.vector.memset(o[0], x), [o], [])

    def act(o, i, fn=Fn.Identity, bias=0.0, scale=1.0, acc=None):
        if acc is None:
            issue("a", lambda: g.scalar.activation(o[0], i[0], fn, bias=ap(bias), scale=ap(scale)), [o], [i, bias, scale])
        else:
            issue("a", lambda: g.scalar.activation(o[0], i[0], fn, bias=ap(bias), scale=ap(scale), accum_out=acc[0]),
                  [o, acc], [i, bias, scale])

    def quant(q, s, a, b, tile, at=None):
        at = 4 * a if at is None else at
        o, p, i = V(q, a, b), V(s, a, b), V(tile, at, at + 4 * (b - a))
        issue("v", lambda: g.vector.quantize_mx(o[0], p[0], i[0]), [o, p], [i])

    def mm(bank, lq, ls, at, rq, rs, a, b):
        o = V("ps", 512 * bank, 512 * bank + b - a)
        w, ws, x, xs = V(lq, at, at + 128), V(ls, at, at + 128), V(rq, a, b), V(rs, a, b)
        issue("t", lambda: g.tensor.matmul_mx(o[0], w[0], ws[0], x[0], xs[0], True, True), [o], [w, ws, x, xs])

    def iota(o, pattern, base, cm):
        if SCRATCH[o[1]][2] == I:
            issue("g", lambda: g.iota(o[0], pattern, base, cm), [o], [])
        else:
            issue("g", lambda: g.iota(o[0], pattern, base, cm, allow_small_or_imprecise_dtypes=True), [o], [])

    def dma(q, out, in_, outs, ins):
        ndma[0] += 1
        issue(q, lambda: eng[q].dma_start(out, in_), outs, ins, sem="dma%d" % (ndma[0] - 1), inc=16)

    def send(dst, to, src, sem, codes=False):
        rid, pid = topo.addr(dst, core)
        mask, n = topo.mask(core, dst), len(topo.engines(core, dst))
        o, i = (to[0].bitcast(dt.uint8), src[0].bitcast(dt.uint8)) if codes else (to[0], src[0])
        issue("g", lambda: g.remote_dma(o, i, T.sem[sem], T.sem.sent, pid, rid, mask), [], [src], sem="sent", inc=n, direct=True)

    def arrives(sem, total, views):
        count[sem] = total
        events.append((sem, total, {}))
        for v in views:
            wr[v[1]][v[2]] = len(events) - 1

    def col(i):
        return V("col", i, i + 1)

    def coli(i):
        return V("coli", i, i + 1)

    def L(name, i, n=1):
        return V(name, K * i, K * (i + n))

    def diag(name):
        return V(name, 15, C, 16)

    dma("s", T.szi[:], T.sz[:], [V("szi")], [])
    dma("a", T.xt[:], T.x[:], [V("xt")], [])
    dma("s", T.pri[:], T.pr[:], [V("pri")], [])
    dma("s", T.ut[:], T.u[:], [V("ut")], [])
    dma("s", T.qw[:].bitcast(dt.uint8), T.wc[:], [V("qw")], [])
    dma("s", T.sw[:], T.ws[:], [V("sw")], [])
    dma("s", T.vt[:], T.v[:], [V("vt")], [])

    iw = V("iot")
    iota(coli(0), [[0, 1]], 0, 1)
    iota(L("cst", 0), [[16, K]], 0, 0)
    iota(V("m16"), [[1, 16]], 0, 0)
    iota(iw, [[1, 360]], 0, 0)
    iota(V("iw2"), [[4, 354], [1, 2]], 0, 0)
    iota(V("col", 24, 28), [[1, 2], [32, 2]], 0, 0)
    iota(V("m8"), [[0, 92], [1, 8]], 0, 0)
    iota(V("td"), [[0, SL]], 0, 0)
    fill(V("ones"), 1.0)
    fill(V("twos"), -2.0)
    act(V("bt", 0, SL, 4), V("ones", 0, 354), scale=0.0)
    act(V("bt", 1, SL, 4), V("ones", 0, 354), scale=0.0)
    fill(V("r8", 8, 16), 2.0)
    ts(coli(1), coli(0), 15, Op.bitwise_and)
    ts(coli(2), coli(0), 7, Op.bitwise_and)
    ts(coli(3), coli(0), 3, Op.arith_shift_right, 1, Op.bitwise_and)
    ts(coli(4), coli(0), 4, Op.arith_shift_right)
    scan(V("r8", 0, 8), V("r8", 8, 16), V("ones", 0, 8), 0.5, Op.mult, Op.add)
    cp(V("col", 0, 3), V("coli", 1, 4))
    tt(coli(5), coli(4), coli(0), Op.add)
    nL = L("cst", 1)
    nbias, dum, n4, evn, koff, kthr, nk, dep = (L("cst", i) for i in (2, 3, 4, 5, 6, 7, 8, 9))
    szu, paru, endu, e1u, depu, pmu = (L("su16", i) for i in range(6))
    pick, rep = V("su16", 6 * K, 6 * K + 4), V("su16", 7 * K, 7 * K + 8)
    fill(V("pp", 0, 1), 1.0)
    fill(V("pq", 0, 1), 1.0)
    ts(V("r8", 16, 24), V("m16", 0, 8), col(1), Op.is_equal)
    ts(nL, L("cst", 0), col(0), Op.add)
    ts(col(9), col(2), -2.0, Op.mult, 5.0, Op.add)
    ts(col(10), col(2), 4.0, Op.mult)
    tt(V("r8", 24, 32), V("r8", 0, 8), V("r8", 16, 24), Op.mult)
    ts(col(11), col(2), 6.0, Op.mult)
    ts(V("r8", 32, 48), V("m16"), col(0), Op.subtract)
    ts(pmu, L("cst", 0), 0.0, Op.mult, col(0), Op.add)
    issue("v", lambda: g.vector.tensor_reduce(col(5)[0], V("r8", 24, 32)[0], AxisListType.X, Op.add), [col(5)], [V("r8", 24, 32)])
    ts(V("r8", 48, 64), V("r8", 32, 48), 0.0, Op.is_equal, 4 * BIG, Op.mult)
    ts(V("r8", 64, 80), V("r8", 32, 48), 1.0, Op.is_equal, -BIG, Op.mult)
    act(V("n2"), V("iot", 0, C), scale=col(10), bias=col(11))
    act(nbias, nL, scale=-1.0, bias=-0.5)
    ts(col(12), col(0), 15.0, Op.is_lt, BIG, Op.mult)
    ts(col(6), col(5), -1.5, Op.mult)
    tt(V("m16"), V("r8", 48, 64), V("r8", 64, 80), Op.add)
    ts(col(15), col(0), 0.5, Op.mult, -8.0, Op.add)
    cp(rep, V("cst", 0, 8))
    ts(col(7), col(5), 0.5, Op.mult)
    act(col(8), col(9), scale=4096.0)
    act(col(13), col(12), scale=-1.0 / 64, bias=-4.0)
    act(col(16), col(5), bias=-0.5)
    act(col(18), col(5), scale=-4.0)
    act(koff, nL, scale=0.5, bias=col(15))
    act(V("dmb"), X(V("m16"), pmu), scale=1.0 / 64)

    cp(szu, V("szi"))
    tt(V("csti"), V("szi"), nL, Op.add)
    ts(L("cst", 10), V("pri"), 1.0, Op.add)
    ts(L("cst", 11), V("pri"), 2.0, Op.mult, 4.0, Op.add)
    cp(paru, V("pri"))
    act(V("r2"), X(iw, szu), Fn.Abs, bias=col(6))
    act(V("r3"), X(iw, szu))
    tt(L("cst", 10), L("cst", 10), nL, Op.not_equal)
    cp(endu, V("csti"))
    act(V("r5"), X(iw, endu))
    ts(L("cst", 12), V("szi"), col(5), Op.is_ge, col(9), Op.mult)
    tt(L("cst", 11), L("cst", 11), L("cst", 10), Op.add)
    ts(L("cst", 13), V("szi"), 0.5, Op.mult, col(5), Op.is_le)
    ts(coli(6), coli(5), 1, Op.bitwise_and)
    cp(e1u, L("cst", 11))
    tt(L("cst", 12), L("cst", 12), L("cst", 13), Op.mult)
    quant("qu", "su", 0, 128, "ut")
    tt(V("r4"), X(V("iw2"), e1u), V("n2"), Op.max)
    cp((T.qr[:].bitcast(dt.uint32), "qr", np.arange(128)), X((T.qu[:].bitcast(dt.uint32), "qu", np.arange(128)), rep))
    cp(V("sr"), X(V("su"), rep))
    ts(V("r1"), V("r2"), col(7), Op.is_le, 1.0 / 4096, Op.mult)
    quant("qx0", "sx0", 0, C, "xt")
    act(V("ops"), V("r1"), bias=-4.0, scale=col(8))
    act(V("r6"), V("r2"), Fn.Relu, scale=8.0, bias=col(18))
    mm(4, "qr", "sr", 0, "qx0", "sx0", 0, C)
    tt(V("mm"), X(V("r1"), paru), V("r4"), Op.mult)
    act(V("hold"), X(V("r3"), paru), Fn.Sign, scale=-1.0, bias=col(16))
    at = 0
    for c in range(K):
        n = 16 * (c + 1)
        act(V("junk", at, at + n), V("r5", 0, n), Fn.Sign, bias=V("cst", 2 * K + c, 2 * K + c + 1),
            acc=V("cst", 14 * K + c, 14 * K + c + 1))
        at += n
    act(dum, nL, bias=float(SL))
    act(n4, nL, scale=4.0, bias=6.0)
    act(evn, nL, scale=4.0, bias=7.0)
    act(nk, nL, scale=4.0)
    act(col(14), col(12), scale=0.625)
    for o, x in ((V("nn", 0, 32), 4.0), (V("nn", 32, 64), 6.0), (V("jj", 0, 1), 0.0), (V("bt", 2, 4), 0.0),
                 (V("bt", SL - 2, SL), 0.0), (V("xp", C, 4 * PL, PL), 0.0), (V("yp", C, 4 * PL, PL), 0.0),
                 (V("fo", 192, 4 * 208, 208), 0.0)):
        act(o, V("ones", 0, len(o[2])), scale=x)
    act(V("nf"), V("iot", 0, C), scale=1.0 / 1024)

    def more_constants():
        iota(V("vtb"), [[1, C], [0, 4]], C + 1, 0)
        iota(V("vtb", 0, 4 * C, 4), [[1, C]], 0, 0)
        issue("g", lambda: g.affine_select(T.ew[:], T.ones[:], [[-1, 520]], Op.is_equal, 0.0, 3, 4), [V("ew")], [V("ones")])
        iota(V("io2", 0, 706), [[0, 2], [1, C + 1]], 0, 0)

    def depth_tables():
        act(V("r2"), X(iw, depu))
        act(V("dm"), X(V("m16"), pmu))
        act(V("td", 8, SL, 4), V("r2"), scale=-2.0, bias=-2.0)
        act(V("td", 9, SL, 4), V("r2"), scale=-2.0, bias=-2.0)
        act(V("c2t", 0, 4 * C, 4), V("r2"), scale=0.0, bias=-OFF)
        act(V("c2t", 1, 4 * C, 4), V("r2"), bias=1.0 - OFF)
        act(V("c2t", 2, 4 * C, 4), V("r2"), bias=2.0 - OFF)
        act(V("c2t", 3, 4 * C, 4), V("r2"), scale=0.0, bias=-OFF)

    def defects(bank, a, b):
        ts(V("bb", a, b), V("ps", 512 * bank, 512 * bank + b - a), 0.0, Op.is_gt, 0.5, Op.subtract)

    def shifts(a, b):
        tt(V("hh", a, b), V("bb", a, b), V("ops", a, b), Op.add)

    def plane(name, b, src):
        o, i = V(name, PL * b + C + 1, PL * b + 2 * C + 1), V(name, PL * b, PL * b + C)
        act(i, src)
        dma("s", o[0], i[0], [o], [i])

    def xplane(b):
        plane("xp", b, V("xt", b, 4 * C, 4))

    def result(a, b, bank):
        cp(V("yo", a, b), V("ps", 512 * bank, 512 * bank + b - a))
        dma("s" if a else "a", T.y[:, a:b], T.yo[:, a:b], [], [V("yo", a, b)])

    def layer(t, a, b, src, fbuf, fw, flist, olist, bank, first=None, meanwhile=None):
        n, nf = b - a, 16 * len(flist[2])
        for p in range(4):
            act(V(fbuf, fw * p, fw * p + nf), X(V(src, PL * p, PL * p + C + 1), flist))
        for p in range(4):
            tt(V("zt", 4 * a + p, 4 * b, 4), X(V(src, PL * p, PL * p + 2 * C + 1), olist), V(fbuf, fw * p + 1, fw * p + 1 + n), Op.subtract)
            if p < 3:
                act(V("z128", C * p + a, C * p + b), V("zt", 4 * a + p, 4 * b, 4), scale=128.0)
            if p == 1 and first:
                first()
        quant("qz", "zs", a, b, "zt")
        for p in (3, 0, 1, 2):
            mm(p, "qw", "sw", 128 * p, "qz", "zs", a, b)
        act(V("tf", 3 * C + a, 3 * C + b), V("ps", 1536, 1536 + n), scale=0.0078125)
        if meanwhile:
            meanwhile()
        for p in range(3):
            tt(V("tf", C * p + a, C * p + b), V("ps", 512 * p, 512 * p + n), V("z128", C * p + a, C * p + b), Op.add)
            act(V("xt", 4 * a + p, 4 * b, 4), V("tf", C * p + a, C * p + b), scale=0.0078125)
        tt(V("xt", 4 * a + 3, 4 * b, 4), V("tf", 3 * C + a, 3 * C + b), V("zt", 4 * a + 3, 4 * b, 4), Op.add)
        qx, sx = "qx%d" % (t + 1), "sx%d" % (t + 1)
        quant(qx, sx, a, b, "xt")
        if t + 1 < R:
            mm(bank, "qr", "sr", 0, qx, sx, a, b)
        else:
            mm(bank, "qv", "sv", 0, qx, sx, a, b)
            dma("s", T.oc[:, 4 * a:4 * b], T[qx][:, a:b].bitcast(dt.uint8), [], [V(qx, a, b)])

    def evens(i):
        a, b = 88 * i, 88 * i + 88
        scan(V("ee", a, b), V("oo", a, b), V("ones", a, b), V("ee", a - 1, a) if i else 0.0, Op.add, Op.add)
        if i == 3:
            act(col(17), V("ee", C - 1, C), scale=-0.5, bias=float(C))
            act(V("jj", C + 1, 2 * C + 1), V("ee"), scale=0.5, bias=col(17))

    defects(4, 0, C)
    ts(kthr, L("cst", 12), col(13), Op.add)
    ts(col(3), coli(6), 46.0, Op.mult)
    for t in range(R):
        dst = T.cores[(rank + STEP[t]) % N]
        src = T.cores[(rank - STEP[t]) % N]
        ne = len(topo.engines(src, core))
        qx, sx, lq, ls, ll, lo = ("%s%d" % (k, t) for k in ("qx", "sx", "lq", "ls", "ll", "lo"))
        send(dst, V(lq), V(qx), "big%d" % t, codes=True)
        send(dst, V(ls), V(sx), "big%d" % t)
        arrives("big%d" % t, 2 * ne, [V(lq), V(ls)])
        arrives("lst%d" % t, ne, [V(ll)])
        if t == 0:
            more_constants()
        else:
            for b in range(4):
                xplane(b)

        scan(V("pp", 1, C + 1), V("bb"), V("twos"), 1.0, Op.mult, Op.mult)
        scan(V("pq", 1, C), V("bb", 0, C - 1), V("twos", 0, C - 1), 1.0, Op.mult, Op.mult)
        if t == 0:
            shifts(0, C)
        tt(V("oo"), X(V("pp", 0, C + 1), endu), V("pq", 0, C), Op.mult)
        if t == 0:
            tt(V("d0"), V("r6"), V("mm"), Op.max)
        else:
            shifts(0, A)
        tt(V("d1"), V("oo"), V("hh"), Op.add)
        evens(0)
        if t == 0:
            ts(col(4), col(0), 2.0, Op.mult, col(3), Op.add)
        scan(V("vv"), V("d0"), V("d1"), 0.0, Op.min, Op.max)
        scan(V("wd"), V("dmb"), V("d1"), 0.0, Op.add, Op.min)
        tt(V("gg"), X(V("vv"), paru), V("mm"), Op.min)
        s = [L("sl", i) for i in range(24)]
        kind, nbot, even, y, t5, m, rise, fall, br, bs = s[:10]
        tt(kind, diag("wd"), kthr, Op.subtract)
        if t == 0:
            xplane(0)
            ts(dep, L("cst", 14), 0.5, Op.mult)
            ts(V("uu", 0, 16), V("ones", 0, 16), 0.0, Op.mult)
            ts(V("uu", 368, 384), V("ones", 0, 16), 0.0, Op.mult)
        evens(1)
        if t == 0:
            tt(dep, dep, koff, Op.add)
        scan(V("uu", 16, 16 + C), V("hold"), V("gg"), 0.0, Op.mult, Op.max)
        if t == 0:
            cp(depu, dep)
            depth_tables()
        ts(nbot, kind, -0.5, Op.not_equal, 4096.0, Op.mult)
        ts(even, kind, 0.0, Op.is_gt, 4096.0, Op.mult)
        for o, i in ((V("tt", 0, C), V("uu", 16, 16 + C)), (V("tt", C, 736), V("uu"))):
            issue("v", lambda: g.vector.transpose(o[0], i[0]), [o], [i])
        evens(2)
        if t == 0:
            ts(pick, V("col", 24, 28), col(4), Op.add, 91.0, Op.min)
        scan(V("rr"), V("m8"), V("tt"), 0.0, Op.min, Op.max)
        evens(3)
        ts(s[16], even, 3.0, Op.min)
        ts(V("r8", 0, 92), V("rr", 7, 736, 8), 4096.0, Op.mult)
        if t == 0:
            tt(V("pay"), X(iw, depu), V("nf"), Op.add)
        tt(s[16], s[16], nk, Op.add)
        tt(V("zi"), X(V("r8", 0, 92), pick), V("nn"), Op.max)
        if t == 0:
            tt(V("bt", 6, SL - 2, 4), V("nf"), V("r2"), Op.subtract)
            act(V("bt", 7, SL - 1, 4), V("bt", 6, SL - 2, 4), bias=353.0 / 1024 - 1)
            xplane(1)
        e, t4, es = V("zi", 0, K), V("zi", 32, 32 + K), L("sli", 0)
        ts(es, e, 2044, Op.bitwise_and)
        tt(t5, t4, even, Op.add)
        tt(y, e, nbot, Op.add)
        ts(s[17], e, 1.0, Op.add)
        tt(m, t5, es, Op.max)
        tt(bs, t5, n4, Op.is_equal)
        tt(L("lb", 0), y, dum, Op.min)
        tt(br, y, m, Op.is_equal)
        tt(s[11], bs, e, Op.mult)
        tt(L("lb", 2), m, evn, Op.min)
        tt(s[12], br, s[17], Op.mult)
        tt(fall, e, m, Op.is_gt)
        tt(s[16], s[16], bs, Op.add)
        tt(L("lb", 1), s[11], s[12], Op.max)
        ts(s[18], br, 2.0, Op.mult)
        tt(rise, e, m, Op.is_equal)
        cp(L("lu", 0, 3), L("lb", 0, 3))
        tt(L("lb", 4), fall, e, Op.mult)
        tt(L("lb", 3), s[16], s[18], Op.add)
        act(V("c1"), X(V("td"), L("lu", 1)), bias=OFF)
        if t == 0:
            xplane(2)
            xplane(3)
        cp(X(V("bt"), L("lu", 0)), V("pay"))
        act(V("gb"), X(V("bt", 0, SL), L("lu", 2)))
        cp(L("lu", 3, 2), L("lb", 3, 2))
        ts(s[13], rise, -2.0, Op.mult, 1.0, Op.add)
        tt(V("ga"), X(V("bt", 0, SL), L("lu", 1)), V("c1"), Op.add)
        act(V("c2"), X(V("c2t"), L("lu", 3)))
        act(V("c3"), X(V("td"), L("lu", 4)))
        act(V("vr"), X(V("vtb"), L("lu", 3)))
        tt(s[13], s[13], dep, Op.mult)
        scan(V("w"), V("dm"), V("gb"), 0.0, Op.add, Op.min)
        tt(s[13], s[13], fall, Op.add)
        if t == 0:
            quant("qe", "se", 0, 128, "ew", 3)
        ts(L("sli", 1), diag("w"), col(12), Op.add, 1024.0, Op.mult)
        scan(V("jj", 1, 177), V("ga", 0, 176), V("c2", 0, 176), 0.0, Op.add, Op.add)
        ts(L("sli", 2), L("sli", 1), 1023, Op.bitwise_and)
        ts(L("sli", 3), L("sli", 1), 10, Op.arith_shift_right)
        scan(V("jj", 177, C + 1), V("ga", 176, C), V("c2", 176, C), V("jj", 176, 177), Op.add, Op.add)
        cp(L("lu", 5), L("sli", 2))
        tt(s[14], s[13], L("sli", 3), Op.add)
        if t == 0:
            act(V("dmh"), X(V("m16"), pmu), scale=0.625)
            quant("qe", "se", 128, 256, "ew", 2)
        tt(V("gf"), X(V("jj", 0, 2 * C + 1), L("lu", 5)), V("c3"), Op.add)
        if t == 0:
            quant("qe", "se", 256, 384, "ew", 1)
        scan(V("wh"), V("dmh"), V("gf"), 0.0, Op.add, Op.min)
        if t == 0:
            quant("qe", "se", 384, 512, "ew", 0)
        for b in range(4):
            mm(b, "qe", "se", 128 * b, lq, ls, 0, C)
            plane("yp", b, V("ps", 512 * b, 512 * b + C))
        tt(s[15], diag("wh"), s[14], Op.add)
        if t == 0:
            quant("qv", "sv", 0, 128, "vt")
        ts(L("lu", 6), s[15], col(14), Op.add)
        cp(X(V("vo"), L("lu", 6)), V("vr"))
        scan(V("w"), V("dm"), V("vo"), 0.0, Op.add, Op.min)
        ts(L(lo, 0), diag("w"), col(12), Op.add, float(C), Op.min)
        ts(L(lo, 1), diag("w"), col(12), Op.add)
        send(dst, V(ll), V(lo, 0, 32), "lst%d" % t)
        layer(t, A, C, "xp", "fo", 208, V(lo, 10, K), V(lo, K + 10, 2 * K), 4)
        if t + 1 < R:
            layer(t, 0, A, "yp", "fl", 176, V(ll, 0, 11), V(ll, K, K + 10), 5, lambda: defects(4, A, C), lambda: shifts(A, C))
            defects(5, 0, A)
        else:
            layer(t, 0, A, "yp", "fl", 176, V(ll, 0, 11), V(ll, K, K + 10), 5, None, lambda: result(A, C, 4))
            act(V("otr"), X(V("io2", 0, 706), L(lo, 1)))
            dma("s", T.ot[:], T.otr[0:128:16, :], [], [V("otr")])
            sx = "sx%d" % R
            for k in range(4):
                dma("sa"[k % 2], T.osc[4 * k:4 * k + 4, :], T[sx][32 * k:32 * k + 4, :], [], [V(sx)])
            result(0, A, 5)

    for sem, n in count.items():
        g.wait_ge(T.sem[sem], n)
